import numpy as np
import ml_dtypes


def mxq(x, axis, fmt="e4m3"):
    dtype, down = {"e4m3": (ml_dtypes.float8_e4m3fn, 7), "e5m2": (ml_dtypes.float8_e5m2, 14)}[fmt]
    v = np.moveaxis(np.asarray(x, np.float32).astype(ml_dtypes.bfloat16).astype(np.float64), axis, -1)
    blocks = v.reshape(v.shape[:-1] + (-1, 32))
    amax = np.abs(blocks).max(-1, keepdims=True)
    byte = np.maximum(np.where(amax > 0, np.frexp(amax)[1] - 1 + 127, 0) - down, 1)
    scale = np.exp2(byte - 127.0)
    codes = (blocks / scale).astype(np.float32).astype(dtype).astype(np.float64)
    return np.moveaxis((codes * scale).reshape(v.shape), -1, axis)


WIDE = False


def mx_kscale(k):
    if not WIDE:
        return np.ones(k)
    levels = np.array([10, -10, 5, -5, 0])
    if k % 512:
        return np.exp2(np.random.permutation(np.resize(levels, k // 32))).repeat(32)
    a = np.empty((k // 512, 16))
    for p in range(k // 512):
        a[p, :8] = np.random.permutation(np.resize(levels, 8))
        for g in range(8):
            far = levels[np.abs(levels - a[p, g]) >= 10]
            a[p, g + 8] = far[np.random.randint(len(far))]
    return np.exp2(a.ravel()).repeat(32)


def f64(x):
    return np.asarray(x).astype(np.float64)


def striped(idx):
    return np.tile(idx.reshape(-1, 16).T, (8, 1)).astype(np.uint16)


def unstriped(offs):
    return offs[:16].T.reshape(-1).astype(np.int64)


E2M1 = np.array([0.0, 0.5, 1.0, 1.5, 2.0, 3.0, 4.0, 6.0, -0.0, -0.5, -1.0, -1.5, -2.0, -3.0, -4.0, -6.0])


def pack_fp4(w):
    k, n = w.shape
    w = f64(np.asarray(w, np.float32).astype(ml_dtypes.bfloat16)).reshape(k // 32, 32, n)
    amax = np.abs(w).max(1)
    mant, ex = np.frexp(amax / 6.0)
    byte = np.clip(np.where(amax > 0, np.where(mant > 0.5, ex, ex - 1) + 127, 1), 1, 254)
    scaled = (w * np.exp2(127.0 - byte)[:, None, :]).reshape(k, n).astype(np.float32)
    c = np.ascontiguousarray(scaled.reshape(k // 512, 128, 4, n).transpose(0, 1, 3, 2)).astype(ml_dtypes.float4_e2m1fn).view(np.uint8) & 0xF
    words = (c[..., 0::2] | (c[..., 1::2] << 4)).reshape(k // 512, 128, 2 * n)
    return np.ascontiguousarray(words), np.ascontiguousarray(byte.astype(np.uint8).reshape(k // 512, 16, n))


def unpack_fp4(words, scales):
    g, _, n = scales.shape
    words = np.ascontiguousarray(words).reshape(g, 128, n, 2)
    nib = np.empty((g, 128, n, 4), np.uint8)
    nib[..., 0::2] = words & 0xF
    nib[..., 1::2] = words >> 4
    vals = E2M1[nib] * np.repeat(np.exp2(scales.astype(np.float64) - 127.0), 8, axis=1)[..., None]
    return vals.transpose(0, 1, 3, 2).reshape(g * 512, n)


K, T, S, N = 512, 4096, 1024, 128
P = 2 ** 7


def setup_inputs():
    n = np.random.standard_normal
    s = mx_kscale(K)[:, None]
    packed_w1 = pack_fp4(n((K, N)) / np.sqrt(K) / s)
    return {
        "xT": (n((K, T)) * s).astype(np.float32),
        "zp": np.tile(np.random.uniform(-0.6, 0.6, T), (P, 1)).astype(np.float32),
        "csum": n((N, 1)).astype(np.float32),
        "w1_words": packed_w1[0],
        "w1_scales": packed_w1[1],
        "offs": striped(np.random.permutation(T)[:S]),
    }


def reference(xT, zp, csum, w1_words, w1_scales, offs):
    xq = mxq(f64(xT)[:, unstriped(offs)], 0, "e4m3")
    y = unpack_fp4(w1_words, w1_scales).T @ xq
    zg = f64(zp)[:1][:, unstriped(offs)]
    return y - (f64(csum) * zg)

@@ -1,0 +1,123 @@
+from contextlib import ExitStack
+
+import concourse.mybir as mybir
+from concourse.masks import make_identity
+
+K, T, S, N = 512, 4096, 1024, 128
+FLOPS = 2 * K * N * S
+
+F32 = mybir.dt.float32
+BF16 = mybir.dt.bfloat16
+I32 = mybir.dt.int32
+U32 = mybir.dt.uint32
+U16 = mybir.dt.uint16
+U8 = mybir.dt.uint8
+FP8X4 = mybir.dt.float8_e4m3fn_x4
+FP4X4 = mybir.dt.float4_e2m1fn_x4
+COPY = mybir.ActivationFunctionType.Copy
+
+P = 128
+PACK = 4
+HALF = S // 2
+ZP_COLS = T // P
+BANK_SLOTS = 4
+PIECE = 256
+LAST_CHUNKS = ((1024, "scalar"), (1024, "scalar"), (1024, "vector"), (512, "scalar"), (512, "scalar"))
+
+
+def tile_picked_zeropt_none_l_kernel(tc, xT, zp, csum, w1_words, w1_scales, offs, out):
+    nc = tc.nc
+    with ExitStack() as ctx:
+        keep = ctx.enter_context(tc.tile_pool(name="keep", bufs=1))
+        zbanks = ctx.enter_context(tc.psum_pool(name="zbanks", bufs=4))
+        ybanks = ctx.enter_context(tc.psum_pool(name="ybanks", bufs=1))
+
+        offsets = keep.tile([P, S // 16], U16, name="offsets")
+        nc.sync.dma_start(offsets[:], offs)
+        half_offsets = [offsets[:, h * (HALF // 16) : (h + 1) * (HALF // 16)] for h in range(2)]
+
+        zp_cut = keep.tile([P, ZP_COLS], F32, name="zp_cut")
+        nc.scalar.dma_start(out=zp_cut[:], in_=zp[0:1, :].rearrange("o (p c) -> (o p) c", c=ZP_COLS))
+
+        rows = xT.rearrange("(p t) w -> p t w", t=PACK)
+        planes = [keep.tile([P, T], F32, name=f"plane{t}") for t in range(PACK)]
+        for t in range(PACK - 1):
+            nc.sync.dma_start(out=planes[t][:], in_=rows[:, t, :])
+        last = PACK - 1
+        chunks = []
+        c0 = 0
+        for width, engine in LAST_CHUNKS:
+            chunks.append((slice(c0, c0 + width), engine))
+            c0 = c0 + width
+        for cols, engine in chunks:
+            nc.sync.dma_start(out=planes[last][:, cols], in_=rows[:, last, cols])
+
+        identity = keep.tile([P, P], F32, name="identity")
+        make_identity(nc, identity[:])
+
+        w_codes = keep.tile([P, 2 * N], U8, name="w_codes", align_bytes=64)
+        w_scales = keep.tile([P, N], U8, name="w_scales", align_bytes=64)
+        csum_col = keep.tile([P, 1], F32, name="csum_col")
+        nc.gpsimd.memset(w_scales[:].bitcast(I32), 0)
+        nc.scalar.dma_start(out=csum_col[:], in_=csum)
+        nc.gpsimd.dma_start(out=w_codes[:].bitcast(I32), in_=w1_words[0].bitcast(I32))
+        for q in range(4):
+            nc.gpsimd.dma_start(
+                out=w_scales[32 * q : 32 * q + 4, :].bitcast(I32),
+                in_=w1_scales[0, 4 * q : 4 * q + 4, :].bitcast(I32),
+            )
+
+        zp_table = keep.tile([P, T], F32, name="zp_table")
+        zp_runs = zp_table[:].rearrange("p (n a j) -> p a n j", a=ZP_COLS // BANK_SLOTS, j=BANK_SLOTS)
+        for a in range(ZP_COLS // BANK_SLOTS):
+            bank = zbanks.tile([P, BANK_SLOTS, P], F32, name="zbank")
+            for j in range(BANK_SLOTS):
+                c = BANK_SLOTS * a + j
+                nc.tensor.transpose(bank[:, j, :], zp_cut[:, c : c + 1].to_broadcast([P, P]), identity[:])
+            nc.scalar.copy(out=zp_runs[:, a, :, :], in_=bank[:].rearrange("p j n -> p n j"))
+
+        zp_picked = keep.tile([P, S], F32, name="zp_picked")
+        nc.vector.tensor_copy(zp_picked[:], zp_table[:].indirect(offsets[:]))
+        correction = keep.tile([P, S], F32, name="correction")
+        nc.scalar.activation(correction[:], zp_picked[:], COPY, scale=csum_col[:, 0:1])
+
+        picked = [keep.tile([P, HALF, PACK], BF16, name=f"picked{h}", align_bytes=64) for h in range(2)]
+        for t in range(PACK - 1):
+            for h in (1, 0):
+                nc.vector.tensor_copy(picked[h][:, :, t], planes[t][:].indirect(half_offsets[h]))
+
+        last_bf16 = keep.tile([P, T], BF16, name="last_bf16")
+        for cols, engine in chunks:
+            if engine == "scalar":
+                nc.scalar.copy(out=last_bf16[:, cols], in_=planes[last][:, cols])
+            else:
+                nc.vector.tensor_copy(out=last_bf16[:, cols], in_=planes[last][:, cols])
+        nc.vector.tensor_copy(picked[0][:, :, last], planes[last][:].indirect(half_offsets[0]))
+        nc.scalar.activation(picked[1][:, :, last], last_bf16[:].indirect(half_offsets[1]), COPY)
+
+        sums = []
+        for i in range(S // PIECE):
+            h, first = divmod(i * PIECE, HALF)
+            x_codes = keep.tile([P, PIECE], U32, name=f"x_codes{i}", align_bytes=64)
+            x_scales = keep.tile([P, PIECE], U8, name=f"x_scales{i}", align_bytes=64)
+            nc.vector.quantize_mx(
+                out=x_codes[:].bitcast(FP8X4),
+                scales=x_scales[:],
+                in_=picked[h][:, first : first + PIECE, :].rearrange("p c t -> p (c t)"),
+            )
+            y = ybanks.tile([P, PIECE], F32, name=f"y{i}")
+            nc.tensor.matmul_mx(
+                out=y[:],
+                lhsT=w_codes[:].bitcast(FP4X4),
+                lhsT_scale=w_scales[:],
+                rhs=x_codes[:].bitcast(FP8X4),
+                rhs_scale=x_scales[:],
+                start=True,
+                stop=True,
+            )
+            sums.append(y)
+        for i in range(S // PIECE):
+            cols = slice(i * PIECE, (i + 1) * PIECE)
+            result = keep.tile([P, PIECE], F32, name=f"result{i}")
+            nc.vector.tensor_tensor(result[:], sums[i][:], correction[:, cols], mybir.AluOpType.subtract)
+            nc.sync.dma_start(out=out[:, cols], in_=result[:])

@@ -22,7 +22,7 @@ HALF = S // 2
 ZP_COLS = T // P
 BANK_SLOTS = 4
 PIECE = 256
-LAST_CHUNKS = ((1024, "scalar"), (1024, "scalar"), (1024, "vector"), (512, "scalar"), (512, "scalar"))
+LAST_CHUNKS = ((1024, "scalar"), (1024, "scalar"), (512, "vector"), (768, "scalar"), (512, "vector"), (256, "scalar"))
 
 
 def tile_picked_zeropt_none_l_kernel(tc, xT, zp, csum, w1_words, w1_scales, offs, out):
@@ -33,15 +33,16 @@ def tile_picked_zeropt_none_l_kernel(tc, xT, zp, csum, w1_words, w1_scales, offs
         ybanks = ctx.enter_context(tc.psum_pool(name="ybanks", bufs=1))
 
         offsets = keep.tile([P, S // 16], U16, name="offsets")
-        nc.sync.dma_start(offsets[:], offs)
         half_offsets = [offsets[:, h * (HALF // 16) : (h + 1) * (HALF // 16)] for h in range(2)]
 
         zp_cut = keep.tile([P, ZP_COLS], F32, name="zp_cut")
-        nc.scalar.dma_start(out=zp_cut[:], in_=zp[0:1, :].rearrange("o (p c) -> (o p) c", c=ZP_COLS))
+        nc.sync.dma_start(out=zp_cut[:], in_=zp[0:1, :].rearrange("o (p c) -> (o p) c", c=ZP_COLS))
 
         rows = xT.rearrange("(p t) w -> p t w", t=PACK)
         planes = [keep.tile([P, T], F32, name=f"plane{t}") for t in range(PACK)]
-        for t in range(PACK - 1):
+        nc.sync.dma_start(out=planes[0][:], in_=rows[:, 0, :])
+        nc.sync.dma_start(offsets[:], offs)
+        for t in range(1, PACK - 1):
             nc.sync.dma_start(out=planes[t][:], in_=rows[:, t, :])
         last = PACK - 1
         chunks = []
@@ -59,13 +60,13 @@ def tile_picked_zeropt_none_l_kernel(tc, xT, zp, csum, w1_words, w1_scales, offs
         w_scales = keep.tile([P, N], U8, name="w_scales", align_bytes=64)
         csum_col = keep.tile([P, 1], F32, name="csum_col")
         nc.gpsimd.memset(w_scales[:].bitcast(I32), 0)
-        nc.scalar.dma_start(out=csum_col[:], in_=csum)
-        nc.gpsimd.dma_start(out=w_codes[:].bitcast(I32), in_=w1_words[0].bitcast(I32))
+        nc.sync.dma_start(out=w_codes[:].bitcast(I32), in_=w1_words[0].bitcast(I32))
         for q in range(4):
-            nc.gpsimd.dma_start(
+            nc.sync.dma_start(
                 out=w_scales[32 * q : 32 * q + 4, :].bitcast(I32),
                 in_=w1_scales[0, 4 * q : 4 * q + 4, :].bitcast(I32),
             )
+        nc.sync.dma_start(out=csum_col[:], in_=csum)
 
         zp_table = keep.tile([P, T], F32, name="zp_table")
         zp_runs = zp_table[:].rearrange("p (n a j) -> p a n j", a=ZP_COLS // BANK_SLOTS, j=BANK_SLOTS)
@@ -78,8 +79,8 @@ def tile_picked_zeropt_none_l_kernel(tc, xT, zp, csum, w1_words, w1_scales, offs
 
         zp_picked = keep.tile([P, S], F32, name="zp_picked")
         nc.vector.tensor_copy(zp_picked[:], zp_table[:].indirect(offsets[:]))
-        correction = keep.tile([P, S], F32, name="correction")
-        nc.scalar.activation(correction[:], zp_picked[:], COPY, scale=csum_col[:, 0:1])
+        zp_negated = keep.tile([P, S], F32, name="zp_negated")
+        nc.scalar.activation(zp_negated[:], zp_picked[:], COPY, scale=-1.0)
 
         picked = [keep.tile([P, HALF, PACK], BF16, name=f"picked{h}", align_bytes=64) for h in range(2)]
         for t in range(PACK - 1):
@@ -118,6 +119,9 @@ def tile_picked_zeropt_none_l_kernel(tc, xT, zp, csum, w1_words, w1_scales, offs
             sums.append(y)
         for i in range(S // PIECE):
             cols = slice(i * PIECE, (i + 1) * PIECE)
-            result = keep.tile([P, PIECE], F32, name=f"result{i}")
-            nc.vector.tensor_tensor(result[:], sums[i][:], correction[:, cols], mybir.AluOpType.subtract)
-            nc.sync.dma_start(out=out[:, cols], in_=result[:])
+            if i == 1:
+                result = picked[1][:].rearrange("p c t -> p (c t)")[:, 0 : 2 * PIECE].bitcast(F32)
+            else:
+                result = keep.tile([P, PIECE], F32, name=f"result{i}")[:]
+            nc.vector.scalar_tensor_tensor(result, zp_negated[:, cols], csum_col[:, 0:1], sums[i][:], mybir.AluOpType.mult, mybir.AluOpType.add)
+            nc.sync.dma_start(out=out[:, cols], in_=result)

@@ -40,9 +40,9 @@ def tile_picked_zeropt_none_l_kernel(tc, xT, zp, csum, w1_words, w1_scales, offs
 
         rows = xT.rearrange("(p t) w -> p t w", t=PACK)
         planes = [keep.tile([P, T], F32, name=f"plane{t}") for t in range(PACK)]
-        nc.sync.dma_start(out=planes[0][:], in_=rows[:, 0, :])
+        nc.sync.dma_start(out=planes[2][:], in_=rows[:, 2, :])
         nc.sync.dma_start(offsets[:], offs)
-        for t in range(1, PACK - 1):
+        for t in range(2):
             nc.sync.dma_start(out=planes[t][:], in_=rows[:, t, :])
         last = PACK - 1
         chunks = []
@@ -68,7 +68,7 @@ def tile_picked_zeropt_none_l_kernel(tc, xT, zp, csum, w1_words, w1_scales, offs
             )
         nc.sync.dma_start(out=csum_col[:], in_=csum)
 
-        zp_table = keep.tile([P, T], F32, name="zp_table")
+        zp_table = keep.tile([P, T], F32, name="zp_table", tag="table_then_picked", align_bytes=64)
         zp_runs = zp_table[:].rearrange("p (n a j) -> p a n j", a=ZP_COLS // BANK_SLOTS, j=BANK_SLOTS)
         for a in range(ZP_COLS // BANK_SLOTS):
             bank = zbanks.tile([P, BANK_SLOTS, P], F32, name="zbank")
@@ -77,17 +77,21 @@ def tile_picked_zeropt_none_l_kernel(tc, xT, zp, csum, w1_words, w1_scales, offs
                 nc.tensor.transpose(bank[:, j, :], zp_cut[:, c : c + 1].to_broadcast([P, P]), identity[:])
             nc.scalar.copy(out=zp_runs[:, a, :, :], in_=bank[:].rearrange("p j n -> p n j"))
 
+        dense = keep.tile([P, S], BF16, name="dense", tag="dense_then_last")
+        nc.vector.tensor_copy(dense[:], planes[2][:].indirect(offsets[:]))
+
         zp_picked = keep.tile([P, S], F32, name="zp_picked")
         nc.vector.tensor_copy(zp_picked[:], zp_table[:].indirect(offsets[:]))
+
+        picked_all = keep.tile([P, S, PACK], BF16, name="picked_all", tag="table_then_picked", align_bytes=64)
+        picked = [picked_all[:, h * HALF : (h + 1) * HALF, :] for h in range(2)]
+        nc.scalar.copy(out=picked_all[:, :, 2], in_=dense[:])
         zp_negated = keep.tile([P, S], F32, name="zp_negated")
         nc.scalar.activation(zp_negated[:], zp_picked[:], COPY, scale=-1.0)
+        for t in range(2):
+            nc.vector.tensor_copy(picked_all[:, :, t], planes[t][:].indirect(offsets[:]))
 
-        picked = [keep.tile([P, HALF, PACK], BF16, name=f"picked{h}", align_bytes=64) for h in range(2)]
-        for t in range(PACK - 1):
-            for h in (1, 0):
-                nc.vector.tensor_copy(picked[h][:, :, t], planes[t][:].indirect(half_offsets[h]))
-
-        last_bf16 = keep.tile([P, T], BF16, name="last_bf16")
+        last_bf16 = keep.tile([P, T], BF16, name="last_bf16", tag="dense_then_last")
         for cols, engine in chunks:
             if engine == "scalar":
                 nc.scalar.copy(out=last_bf16[:, cols], in_=planes[last][:, cols])
@@ -120,7 +124,7 @@ def tile_picked_zeropt_none_l_kernel(tc, xT, zp, csum, w1_words, w1_scales, offs
         for i in range(S // PIECE):
             cols = slice(i * PIECE, (i + 1) * PIECE)
             if i == 1:
-                result = picked[1][:].rearrange("p c t -> p (c t)")[:, 0 : 2 * PIECE].bitcast(F32)
+                result = picked[1].rearrange("p c t -> p (c t)")[:, 0 : 2 * PIECE].bitcast(F32)
             else:
                 result = keep.tile([P, PIECE], F32, name=f"result{i}")[:]
             nc.vector.scalar_tensor_tensor(result, zp_negated[:, cols], csum_col[:, 0:1], sums[i][:], mybir.AluOpType.mult, mybir.AluOpType.add)

@@ -22,7 +22,7 @@ HALF = S // 2
 ZP_COLS = T // P
 BANK_SLOTS = 4
 PIECE = 256
-LAST_CHUNKS = ((1024, "scalar"), (1024, "scalar"), (512, "vector"), (768, "scalar"), (512, "vector"), (256, "scalar"))
+LAST_CHUNKS = ((2048, "scalar"), (1024, "vector"), (768, "vector"), (256, "scalar"))
 
 
 def tile_picked_zeropt_none_l_kernel(tc, xT, zp, csum, w1_words, w1_scales, offs, out):
@@ -42,8 +42,18 @@ def tile_picked_zeropt_none_l_kernel(tc, xT, zp, csum, w1_words, w1_scales, offs
         planes = [keep.tile([P, T], F32, name=f"plane{t}") for t in range(PACK)]
         nc.sync.dma_start(out=planes[2][:], in_=rows[:, 2, :])
         nc.sync.dma_start(offsets[:], offs)
-        for t in range(2):
-            nc.sync.dma_start(out=planes[t][:], in_=rows[:, t, :])
+        nc.sync.dma_start(out=planes[0][:], in_=rows[:, 0, :])
+        w_codes = keep.tile([P, 2 * N], U8, name="w_codes", align_bytes=64)
+        w_scales = keep.tile([P, N], U8, name="w_scales", align_bytes=64)
+        csum_col = keep.tile([P, 1], F32, name="csum_col")
+        nc.gpsimd.memset(w_scales[:].bitcast(I32), 0)
+        nc.sync.dma_start(out=w_codes[:].bitcast(I32), in_=w1_words[0].bitcast(I32))
+        for q in range(4):
+            nc.sync.dma_start(
+                out=w_scales[32 * q : 32 * q + 4, :].bitcast(I32),
+                in_=w1_scales[0, 4 * q : 4 * q + 4, :].bitcast(I32),
+            )
+        nc.sync.dma_start(out=planes[1][:], in_=rows[:, 1, :])
         last = PACK - 1
         chunks = []
         c0 = 0
@@ -56,16 +66,6 @@ def tile_picked_zeropt_none_l_kernel(tc, xT, zp, csum, w1_words, w1_scales, offs
         identity = keep.tile([P, P], F32, name="identity")
         make_identity(nc, identity[:])
 
-        w_codes = keep.tile([P, 2 * N], U8, name="w_codes", align_bytes=64)
-        w_scales = keep.tile([P, N], U8, name="w_scales", align_bytes=64)
-        csum_col = keep.tile([P, 1], F32, name="csum_col")
-        nc.gpsimd.memset(w_scales[:].bitcast(I32), 0)
-        nc.sync.dma_start(out=w_codes[:].bitcast(I32), in_=w1_words[0].bitcast(I32))
-        for q in range(4):
-            nc.sync.dma_start(
-                out=w_scales[32 * q : 32 * q + 4, :].bitcast(I32),
-                in_=w1_scales[0, 4 * q : 4 * q + 4, :].bitcast(I32),
-            )
         nc.sync.dma_start(out=csum_col[:], in_=csum)
 
         zp_table = keep.tile([P, T], F32, name="zp_table", tag="table_then_picked", align_bytes=64)
@@ -123,8 +123,8 @@ def tile_picked_zeropt_none_l_kernel(tc, xT, zp, csum, w1_words, w1_scales, offs
             sums.append(y)
         for i in range(S // PIECE):
             cols = slice(i * PIECE, (i + 1) * PIECE)
-            if i == 1:
-                result = picked[1].rearrange("p c t -> p (c t)")[:, 0 : 2 * PIECE].bitcast(F32)
+            if i < 2:
+                result = picked[1].rearrange("p c t -> p (c t)")[:, 2 * PIECE * i : 2 * PIECE * (i + 1)].bitcast(F32)
             else:
                 result = keep.tile([P, PIECE], F32, name=f"result{i}")[:]
             nc.vector.scalar_tensor_tensor(result, zp_negated[:, cols], csum_col[:, 0:1], sums[i][:], mybir.AluOpType.mult, mybir.AluOpType.add)

@@ -22,7 +22,7 @@ HALF = S // 2
 ZP_COLS = T // P
 BANK_SLOTS = 4
 PIECE = 256
-LAST_CHUNKS = ((2048, "scalar"), (1024, "vector"), (768, "vector"), (256, "scalar"))
+LAST_CHUNKS = ((2048, 1536), (1280, 448), (576, 192), (192, 192))
 
 
 def tile_picked_zeropt_none_l_kernel(tc, xT, zp, csum, w1_words, w1_scales, offs, out):
@@ -47,21 +47,21 @@ def tile_picked_zeropt_none_l_kernel(tc, xT, zp, csum, w1_words, w1_scales, offs
         w_scales = keep.tile([P, N], U8, name="w_scales", align_bytes=64)
         csum_col = keep.tile([P, 1], F32, name="csum_col")
         nc.gpsimd.memset(w_scales[:].bitcast(I32), 0)
+        nc.sync.dma_start(out=planes[1][:], in_=rows[:, 1, :])
+        last = PACK - 1
+        chunks = []
+        c0 = 0
+        for width, scalar_share in LAST_CHUNKS:
+            chunks.append((c0, c0 + scalar_share, c0 + width))
+            c0 = c0 + width
+        for begin, middle, end in chunks:
+            nc.sync.dma_start(out=planes[last][:, begin:end], in_=rows[:, last, begin:end])
         nc.sync.dma_start(out=w_codes[:].bitcast(I32), in_=w1_words[0].bitcast(I32))
         for q in range(4):
             nc.sync.dma_start(
                 out=w_scales[32 * q : 32 * q + 4, :].bitcast(I32),
                 in_=w1_scales[0, 4 * q : 4 * q + 4, :].bitcast(I32),
             )
-        nc.sync.dma_start(out=planes[1][:], in_=rows[:, 1, :])
-        last = PACK - 1
-        chunks = []
-        c0 = 0
-        for width, engine in LAST_CHUNKS:
-            chunks.append((slice(c0, c0 + width), engine))
-            c0 = c0 + width
-        for cols, engine in chunks:
-            nc.sync.dma_start(out=planes[last][:, cols], in_=rows[:, last, cols])
 
         identity = keep.tile([P, P], F32, name="identity")
         make_identity(nc, identity[:])
@@ -92,11 +92,10 @@ def tile_picked_zeropt_none_l_kernel(tc, xT, zp, csum, w1_words, w1_scales, offs
             nc.vector.tensor_copy(picked_all[:, :, t], planes[t][:].indirect(offsets[:]))
 
         last_bf16 = keep.tile([P, T], BF16, name="last_bf16", tag="dense_then_last")
-        for cols, engine in chunks:
-            if engine == "scalar":
-                nc.scalar.copy(out=last_bf16[:, cols], in_=planes[last][:, cols])
-            else:
-                nc.vector.tensor_copy(out=last_bf16[:, cols], in_=planes[last][:, cols])
+        for begin, middle, end in chunks:
+            nc.scalar.copy(out=last_bf16[:, begin:middle], in_=planes[last][:, begin:middle])
+            if middle < end:
+                nc.vector.tensor_copy(out=last_bf16[:, middle:end], in_=planes[last][:, middle:end])
         nc.vector.tensor_copy(picked[0][:, :, last], planes[last][:].indirect(half_offsets[0]))
         nc.scalar.activation(picked[1][:, :, last], last_bf16[:].indirect(half_offsets[1]), COPY)
 

@@ -22,7 +22,7 @@ HALF = S // 2
 ZP_COLS = T // P
 BANK_SLOTS = 4
 PIECE = 256
-LAST_CHUNKS = ((2048, 1536), (1280, 448), (576, 192), (192, 192))
+LAST_CHUNKS = ((2688, 1120), (1088, 352), (320, 320))
 
 
 def tile_picked_zeropt_none_l_kernel(tc, xT, zp, csum, w1_words, w1_scales, offs, out):

@@ -22,7 +22,7 @@ HALF = S // 2
 ZP_COLS = T // P
 BANK_SLOTS = 4
 PIECE = 256
-LAST_CHUNKS = ((2688, 1120), (1088, 352), (320, 320))
+LAST_CHUNKS = ((2880, 960), (960, 288), (256, 256))
 
 
 def tile_picked_zeropt_none_l_kernel(tc, xT, zp, csum, w1_words, w1_scales, offs, out):
@@ -88,8 +88,11 @@ def tile_picked_zeropt_none_l_kernel(tc, xT, zp, csum, w1_words, w1_scales, offs
         nc.scalar.copy(out=picked_all[:, :, 2], in_=dense[:])
         zp_negated = keep.tile([P, S], F32, name="zp_negated")
         nc.scalar.activation(zp_negated[:], zp_picked[:], COPY, scale=-1.0)
-        for t in range(2):
-            nc.vector.tensor_copy(picked_all[:, :, t], planes[t][:].indirect(offsets[:]))
+        nc.vector.tensor_copy(picked_all[:, :, 0], planes[0][:].indirect(offsets[:]))
+        dense_half = keep.tile([P, HALF], BF16, name="dense_half")
+        nc.vector.tensor_copy(dense_half[:], planes[1][:].indirect(half_offsets[1]))
+        nc.scalar.copy(out=picked[1][:, :, 1], in_=dense_half[:])
+        nc.vector.tensor_copy(picked[0][:, :, 1], planes[1][:].indirect(half_offsets[0]))
 
         last_bf16 = keep.tile([P, T], BF16, name="last_bf16", tag="dense_then_last")
         for begin, middle, end in chunks:
@@ -121,10 +124,13 @@ def tile_picked_zeropt_none_l_kernel(tc, xT, zp, csum, w1_words, w1_scales, offs
             )
             sums.append(y)
         for i in range(S // PIECE):
-            cols = slice(i * PIECE, (i + 1) * PIECE)
             if i < 2:
                 result = picked[1].rearrange("p c t -> p (c t)")[:, 2 * PIECE * i : 2 * PIECE * (i + 1)].bitcast(F32)
             else:
                 result = keep.tile([P, PIECE], F32, name=f"result{i}")[:]
-            nc.vector.scalar_tensor_tensor(result, zp_negated[:, cols], csum_col[:, 0:1], sums[i][:], mybir.AluOpType.mult, mybir.AluOpType.add)
-            nc.sync.dma_start(out=out[:, cols], in_=result)
+            step = PIECE // 2 if i == 0 else PIECE
+            for first in range(0, PIECE, step):
+                part = slice(first, first + step)
+                cols = slice(i * PIECE + first, i * PIECE + first + step)
+                nc.vector.scalar_tensor_tensor(result[:, part], zp_negated[:, cols], csum_col[:, 0:1], sums[i][:, part], mybir.AluOpType.mult, mybir.AluOpType.add)
+                nc.sync.dma_start(out=out[:, cols], in_=result[:, part])

@@ -37,70 +37,76 @@ def tile_picked_zeropt_none_l_kernel(tc, xT, zp, csum, w1_words, w1_scales, offs
 
         zp_cut = keep.tile([P, ZP_COLS], F32, name="zp_cut")
         nc.sync.dma_start(out=zp_cut[:], in_=zp[0:1, :].rearrange("o (p c) -> (o p) c", c=ZP_COLS))
+        nc.sync.dma_start(offsets[:], offs)
 
         rows = xT.rearrange("(p t) w -> p t w", t=PACK)
-        planes = [keep.tile([P, T], F32, name=f"plane{t}") for t in range(PACK)]
-        nc.sync.dma_start(out=planes[2][:], in_=rows[:, 2, :])
-        nc.sync.dma_start(offsets[:], offs)
-        nc.sync.dma_start(out=planes[0][:], in_=rows[:, 0, :])
-        w_codes = keep.tile([P, 2 * N], U8, name="w_codes", align_bytes=64)
-        w_scales = keep.tile([P, N], U8, name="w_scales", align_bytes=64)
-        csum_col = keep.tile([P, 1], F32, name="csum_col")
-        nc.gpsimd.memset(w_scales[:].bitcast(I32), 0)
-        nc.sync.dma_start(out=planes[1][:], in_=rows[:, 1, :])
-        last = PACK - 1
+        first_two = keep.tile([P, 2, T], F32, name="first_two")
+        third = keep.tile([P, T], F32, name="third")
+        last = keep.tile([P, T], F32, name="last")
+        nc.sync.dma_start(out=first_two[:], in_=rows[:, 0:2, :])
+        nc.sync.dma_start(out=third[:], in_=rows[:, 2, :])
         chunks = []
         c0 = 0
         for width, scalar_share in LAST_CHUNKS:
             chunks.append((c0, c0 + scalar_share, c0 + width))
             c0 = c0 + width
         for begin, middle, end in chunks:
-            nc.sync.dma_start(out=planes[last][:, begin:end], in_=rows[:, last, begin:end])
+            nc.sync.dma_start(out=last[:, begin:end], in_=rows[:, 3, begin:end])
+
+        w_codes = keep.tile([P, 2 * N], U8, name="w_codes", align_bytes=64)
+        w_scales = keep.tile([P, N], U8, name="w_scales", align_bytes=64)
+        csum_col = keep.tile([P, 1], F32, name="csum_col")
+        nc.gpsimd.memset(w_scales[:].bitcast(I32), 0)
         nc.sync.dma_start(out=w_codes[:].bitcast(I32), in_=w1_words[0].bitcast(I32))
         for q in range(4):
             nc.sync.dma_start(
                 out=w_scales[32 * q : 32 * q + 4, :].bitcast(I32),
                 in_=w1_scales[0, 4 * q : 4 * q + 4, :].bitcast(I32),
             )
+        nc.sync.dma_start(out=csum_col[:], in_=csum)
 
         identity = keep.tile([P, P], F32, name="identity")
         make_identity(nc, identity[:])
 
-        nc.sync.dma_start(out=csum_col[:], in_=csum)
-
-        zp_table = keep.tile([P, T], F32, name="zp_table", tag="table_then_picked", align_bytes=64)
+        zp_table = keep.tile([P, T], F32, name="zp_table", tag="table_then_pairs")
         zp_runs = zp_table[:].rearrange("p (n a j) -> p a n j", a=ZP_COLS // BANK_SLOTS, j=BANK_SLOTS)
         for a in range(ZP_COLS // BANK_SLOTS):
             bank = zbanks.tile([P, BANK_SLOTS, P], F32, name="zbank")
             for j in range(BANK_SLOTS):
                 c = BANK_SLOTS * a + j
                 nc.tensor.transpose(bank[:, j, :], zp_cut[:, c : c + 1].to_broadcast([P, P]), identity[:])
-            nc.scalar.copy(out=zp_runs[:, a, :, :], in_=bank[:].rearrange("p j n -> p n j"))
-
-        dense = keep.tile([P, S], BF16, name="dense", tag="dense_then_last")
-        nc.vector.tensor_copy(dense[:], planes[2][:].indirect(offsets[:]))
+            if a % 2 == 0:
+                nc.scalar.copy(out=zp_runs[:, a, :, :], in_=bank[:].rearrange("p j n -> p n j"))
+            else:
+                nc.vector.tensor_copy(out=zp_runs[:, a, :, :], in_=bank[:].rearrange("p j n -> p n j"))
 
         zp_picked = keep.tile([P, S], F32, name="zp_picked")
         nc.vector.tensor_copy(zp_picked[:], zp_table[:].indirect(offsets[:]))
-
-        picked_all = keep.tile([P, S, PACK], BF16, name="picked_all", tag="table_then_picked", align_bytes=64)
-        picked = [picked_all[:, h * HALF : (h + 1) * HALF, :] for h in range(2)]
-        nc.scalar.copy(out=picked_all[:, :, 2], in_=dense[:])
         zp_negated = keep.tile([P, S], F32, name="zp_negated")
         nc.scalar.activation(zp_negated[:], zp_picked[:], COPY, scale=-1.0)
-        nc.vector.tensor_copy(picked_all[:, :, 0], planes[0][:].indirect(offsets[:]))
-        dense_half = keep.tile([P, HALF], BF16, name="dense_half")
-        nc.vector.tensor_copy(dense_half[:], planes[1][:].indirect(half_offsets[1]))
-        nc.scalar.copy(out=picked[1][:, :, 1], in_=dense_half[:])
-        nc.vector.tensor_copy(picked[0][:, :, 1], planes[1][:].indirect(half_offsets[0]))
 
-        last_bf16 = keep.tile([P, T], BF16, name="last_bf16", tag="dense_then_last")
+        picked = [keep.tile([P, HALF, PACK], BF16, name=f"picked{h}", align_bytes=64) for h in range(2)]
+        picked_words = [picked[h][:].rearrange("p c t -> p (c t)").bitcast(U32).rearrange("p (c u) -> p c u", u=2) for h in range(2)]
+
+        pairs = keep.tile([P, 3, HALF, 2], BF16, name="pairs", tag="table_then_pairs")
+        pair_words = pairs[:].rearrange("p r c e -> p (r c e)").bitcast(U32).rearrange("p (r c) -> p r c", r=3)
+        nc.vector.memset(pair_words[:, 2, :], 0)
+        for h in range(2):
+            for t in range(2):
+                nc.vector.tensor_copy(pairs[:, h, :, t], first_two[:, t, :].indirect(half_offsets[h]))
+            if h == 0:
+                nc.scalar.copy(out=picked_words[0][:, :, 0], in_=pair_words[:, 0, :])
+        nc.vector.tensor_copy(pairs[:, 2, :, 0], third[:].indirect(half_offsets[1]))
+        nc.scalar.copy(out=picked_words[1], in_=pair_words[:, 1:3, :].rearrange("p u c -> p c u"))
+        nc.vector.tensor_copy(picked[0][:, :, 2], third[:].indirect(half_offsets[0]))
+
+        last_bf16 = keep.tile([P, T], BF16, name="last_bf16")
         for begin, middle, end in chunks:
-            nc.scalar.copy(out=last_bf16[:, begin:middle], in_=planes[last][:, begin:middle])
+            nc.scalar.copy(out=last_bf16[:, begin:middle], in_=last[:, begin:middle])
             if middle < end:
-                nc.vector.tensor_copy(out=last_bf16[:, middle:end], in_=planes[last][:, middle:end])
-        nc.vector.tensor_copy(picked[0][:, :, last], planes[last][:].indirect(half_offsets[0]))
-        nc.scalar.activation(picked[1][:, :, last], last_bf16[:].indirect(half_offsets[1]), COPY)
+                nc.vector.tensor_copy(out=last_bf16[:, middle:end], in_=last[:, middle:end])
+        nc.vector.tensor_copy(picked[0][:, :, 3], last[:].indirect(half_offsets[0]))
+        nc.scalar.activation(picked[1][:, :, 3], last_bf16[:].indirect(half_offsets[1]), COPY)
 
         sums = []
         for i in range(S // PIECE):
@@ -125,7 +131,7 @@ def tile_picked_zeropt_none_l_kernel(tc, xT, zp, csum, w1_words, w1_scales, offs
             sums.append(y)
         for i in range(S // PIECE):
             if i < 2:
-                result = picked[1].rearrange("p c t -> p (c t)")[:, 2 * PIECE * i : 2 * PIECE * (i + 1)].bitcast(F32)
+                result = picked[1][:].rearrange("p c t -> p (c t)")[:, 2 * PIECE * i : 2 * PIECE * (i + 1)].bitcast(F32)
             else:
                 result = keep.tile([P, PIECE], F32, name=f"result{i}")[:]
             step = PIECE // 2 if i == 0 else PIECE

@@ -68,8 +68,10 @@ def tile_picked_zeropt_none_l_kernel(tc, xT, zp, csum, w1_words, w1_scales, offs
         identity = keep.tile([P, P], F32, name="identity")
         make_identity(nc, identity[:])
 
-        zp_table = keep.tile([P, T], F32, name="zp_table", tag="table_then_pairs")
-        zp_runs = zp_table[:].rearrange("p (n a j) -> p a n j", a=ZP_COLS // BANK_SLOTS, j=BANK_SLOTS)
+        space = keep.tile([P, T + HALF], F32, name="space")
+        zp_table = space[:, 0:T]
+        nc.gpsimd.memset(space[:, T : T + HALF], 0.0)
+        zp_runs = zp_table.rearrange("p (n a j) -> p a n j", a=ZP_COLS // BANK_SLOTS, j=BANK_SLOTS)
         for a in range(ZP_COLS // BANK_SLOTS):
             bank = zbanks.tile([P, BANK_SLOTS, P], F32, name="zbank")
             for j in range(BANK_SLOTS):
@@ -81,31 +83,33 @@ def tile_picked_zeropt_none_l_kernel(tc, xT, zp, csum, w1_words, w1_scales, offs
                 nc.vector.tensor_copy(out=zp_runs[:, a, :, :], in_=bank[:].rearrange("p j n -> p n j"))
 
         zp_picked = keep.tile([P, S], F32, name="zp_picked")
-        nc.vector.tensor_copy(zp_picked[:], zp_table[:].indirect(offsets[:]))
+        nc.vector.tensor_copy(zp_picked[:], zp_table.indirect(offsets[:]))
         zp_negated = keep.tile([P, S], F32, name="zp_negated")
         nc.scalar.activation(zp_negated[:], zp_picked[:], COPY, scale=-1.0)
 
         picked = [keep.tile([P, HALF, PACK], BF16, name=f"picked{h}", align_bytes=64) for h in range(2)]
         picked_words = [picked[h][:].rearrange("p c t -> p (c t)").bitcast(U32).rearrange("p (c u) -> p c u", u=2) for h in range(2)]
 
-        pairs = keep.tile([P, 3, HALF, 2], BF16, name="pairs", tag="table_then_pairs")
-        pair_words = pairs[:].rearrange("p r c e -> p (r c e)").bitcast(U32).rearrange("p (r c) -> p r c", r=3)
-        nc.vector.memset(pair_words[:, 2, :], 0)
+        pair_space = space[:, T - 3 * HALF : T + HALF]
+        pairs = pair_space.bitcast(BF16).rearrange("p (h u c e) -> p h u c e", h=2, u=2, e=2)
+        pair_words = pair_space.bitcast(U32).rearrange("p (h u c) -> p h c u", h=2, u=2)
+        pair_ints = pair_space.bitcast(I32).rearrange("p (h u c) -> p h c u", h=2, u=2)
         for h in range(2):
             for t in range(2):
-                nc.vector.tensor_copy(pairs[:, h, :, t], first_two[:, t, :].indirect(half_offsets[h]))
-            if h == 0:
-                nc.scalar.copy(out=picked_words[0][:, :, 0], in_=pair_words[:, 0, :])
-        nc.vector.tensor_copy(pairs[:, 2, :, 0], third[:].indirect(half_offsets[1]))
-        nc.scalar.copy(out=picked_words[1], in_=pair_words[:, 1:3, :].rearrange("p u c -> p c u"))
-        nc.vector.tensor_copy(picked[0][:, :, 2], third[:].indirect(half_offsets[0]))
+                nc.vector.tensor_copy(pairs[:, h, 0, :, t], first_two[:, t, :].indirect(half_offsets[h]))
+        nc.vector.tensor_copy(pairs[:, 1, 1, :, 0], third[:].indirect(half_offsets[1]))
+        nc.scalar.copy(out=picked_words[1], in_=pair_words[:, 1])
+        nc.vector.tensor_copy(pairs[:, 0, 1, :, 0], third[:].indirect(half_offsets[0]))
 
         last_bf16 = keep.tile([P, T], BF16, name="last_bf16")
         for begin, middle, end in chunks:
             nc.scalar.copy(out=last_bf16[:, begin:middle], in_=last[:, begin:middle])
             if middle < end:
                 nc.vector.tensor_copy(out=last_bf16[:, middle:end], in_=last[:, middle:end])
-        nc.vector.tensor_copy(picked[0][:, :, 3], last[:].indirect(half_offsets[0]))
+        nc.vector.tensor_copy(pairs[:, 0, 1, :, 1], last[:].indirect(half_offsets[0]))
+        picked_ints = picked[0][:].rearrange("p c t -> p (c t)").bitcast(I32).rearrange("p (c u) -> p c u", u=2)
+        for first in range(0, HALF, PIECE):
+            nc.vector.tensor_copy(out=picked_ints[:, first : first + PIECE, :], in_=pair_ints[:, 0, first : first + PIECE, :])
         nc.scalar.activation(picked[1][:, :, 3], last_bf16[:].indirect(half_offsets[1]), COPY)
 
         sums = []

@@ -35,15 +35,14 @@ def tile_picked_zeropt_none_l_kernel(tc, xT, zp, csum, w1_words, w1_scales, offs
         offsets = keep.tile([P, S // 16], U16, name="offsets")
         half_offsets = [offsets[:, h * (HALF // 16) : (h + 1) * (HALF // 16)] for h in range(2)]
 
-        zp_cut = keep.tile([P, ZP_COLS], F32, name="zp_cut")
-        nc.sync.dma_start(out=zp_cut[:], in_=zp[0:1, :].rearrange("o (p c) -> (o p) c", c=ZP_COLS))
-        nc.sync.dma_start(offsets[:], offs)
-
         rows = xT.rearrange("(p t) w -> p t w", t=PACK)
-        first_two = keep.tile([P, 2, T], F32, name="first_two")
-        third = keep.tile([P, T], F32, name="third")
-        last = keep.tile([P, T], F32, name="last")
-        nc.sync.dma_start(out=first_two[:], in_=rows[:, 0:2, :])
+        planes = [keep.tile([P, T], F32, name=f"plane{t}") for t in range(PACK)]
+        third, last = planes[2], planes[3]
+        zp_cut = keep.tile([P, ZP_COLS], F32, name="zp_cut")
+        nc.sync.dma_start(out=planes[0][:], in_=rows[:, 0, :])
+        nc.sync.dma_start(offsets[:], offs)
+        nc.sync.dma_start(out=zp_cut[:], in_=zp[0:1, :].rearrange("o (p c) -> (o p) c", c=ZP_COLS))
+        nc.sync.dma_start(out=planes[1][:], in_=rows[:, 1, :])
         nc.sync.dma_start(out=third[:], in_=rows[:, 2, :])
         chunks = []
         c0 = 0
@@ -68,19 +67,21 @@ def tile_picked_zeropt_none_l_kernel(tc, xT, zp, csum, w1_words, w1_scales, offs
         identity = keep.tile([P, P], F32, name="identity")
         make_identity(nc, identity[:])
 
-        space = keep.tile([P, T + HALF], F32, name="space")
-        zp_table = space[:, 0:T]
-        nc.gpsimd.memset(space[:, T : T + HALF], 0.0)
+        space = keep.tile([P, S + T], F32, name="space")
+        zp_table = space[:, S : S + T]
+        pair_space = space[:, 0 : 2 * S]
+        pairs = pair_space.bitcast(BF16).rearrange("p (u c e) -> p u c e", u=2, e=2)
+        pair_words = pair_space.bitcast(U32).rearrange("p (u c) -> p c u", u=2)
+        pair_ints = pair_space.bitcast(I32).rearrange("p (u c) -> p c u", u=2)
+        for t in range(2):
+            nc.vector.tensor_copy(pairs[:, 0, :, t], planes[t][:].indirect(offsets[:]))
         zp_runs = zp_table.rearrange("p (n a j) -> p a n j", a=ZP_COLS // BANK_SLOTS, j=BANK_SLOTS)
         for a in range(ZP_COLS // BANK_SLOTS):
             bank = zbanks.tile([P, BANK_SLOTS, P], F32, name="zbank")
             for j in range(BANK_SLOTS):
                 c = BANK_SLOTS * a + j
                 nc.tensor.transpose(bank[:, j, :], zp_cut[:, c : c + 1].to_broadcast([P, P]), identity[:])
-            if a % 2 == 0:
-                nc.scalar.copy(out=zp_runs[:, a, :, :], in_=bank[:].rearrange("p j n -> p n j"))
-            else:
-                nc.vector.tensor_copy(out=zp_runs[:, a, :, :], in_=bank[:].rearrange("p j n -> p n j"))
+            nc.scalar.copy(out=zp_runs[:, a, :, :], in_=bank[:].rearrange("p j n -> p n j"))
 
         zp_picked = keep.tile([P, S], F32, name="zp_picked")
         nc.vector.tensor_copy(zp_picked[:], zp_table.indirect(offsets[:]))
@@ -90,26 +91,19 @@ def tile_picked_zeropt_none_l_kernel(tc, xT, zp, csum, w1_words, w1_scales, offs
         picked = [keep.tile([P, HALF, PACK], BF16, name=f"picked{h}", align_bytes=64) for h in range(2)]
         picked_words = [picked[h][:].rearrange("p c t -> p (c t)").bitcast(U32).rearrange("p (c u) -> p c u", u=2) for h in range(2)]
 
-        pair_space = space[:, T - 3 * HALF : T + HALF]
-        pairs = pair_space.bitcast(BF16).rearrange("p (h u c e) -> p h u c e", h=2, u=2, e=2)
-        pair_words = pair_space.bitcast(U32).rearrange("p (h u c) -> p h c u", h=2, u=2)
-        pair_ints = pair_space.bitcast(I32).rearrange("p (h u c) -> p h c u", h=2, u=2)
-        for h in range(2):
-            for t in range(2):
-                nc.vector.tensor_copy(pairs[:, h, 0, :, t], first_two[:, t, :].indirect(half_offsets[h]))
-        nc.vector.tensor_copy(pairs[:, 1, 1, :, 0], third[:].indirect(half_offsets[1]))
-        nc.scalar.copy(out=picked_words[1], in_=pair_words[:, 1])
-        nc.vector.tensor_copy(pairs[:, 0, 1, :, 0], third[:].indirect(half_offsets[0]))
+        nc.vector.tensor_copy(pairs[:, 1, HALF:S, 0], third[:].indirect(half_offsets[1]))
+        nc.scalar.copy(out=picked_words[1], in_=pair_words[:, HALF:S, :])
+        nc.vector.tensor_copy(pairs[:, 1, 0:HALF, 0], third[:].indirect(half_offsets[0]))
 
         last_bf16 = keep.tile([P, T], BF16, name="last_bf16")
         for begin, middle, end in chunks:
             nc.scalar.copy(out=last_bf16[:, begin:middle], in_=last[:, begin:middle])
             if middle < end:
                 nc.vector.tensor_copy(out=last_bf16[:, middle:end], in_=last[:, middle:end])
-        nc.vector.tensor_copy(pairs[:, 0, 1, :, 1], last[:].indirect(half_offsets[0]))
+        nc.vector.tensor_copy(pairs[:, 1, 0:HALF, 1], last[:].indirect(half_offsets[0]))
         picked_ints = picked[0][:].rearrange("p c t -> p (c t)").bitcast(I32).rearrange("p (c u) -> p c u", u=2)
         for first in range(0, HALF, PIECE):
-            nc.vector.tensor_copy(out=picked_ints[:, first : first + PIECE, :], in_=pair_ints[:, 0, first : first + PIECE, :])
+            nc.vector.tensor_copy(out=picked_ints[:, first : first + PIECE, :], in_=pair_ints[:, first : first + PIECE, :])
         nc.scalar.activation(picked[1][:, :, 3], last_bf16[:].indirect(half_offsets[1]), COPY)
 
         sums = []

@@ -22,7 +22,7 @@ HALF = S // 2
 ZP_COLS = T // P
 BANK_SLOTS = 4
 PIECE = 256
-LAST_CHUNKS = ((2880, 960), (960, 288), (256, 256))
+LAST_CHUNKS = ((384, 384), (2560, 832), (896, 272), (256, 256))
 
 
 def tile_picked_zeropt_none_l_kernel(tc, xT, zp, csum, w1_words, w1_scales, offs, out):
@@ -36,33 +36,37 @@ def tile_picked_zeropt_none_l_kernel(tc, xT, zp, csum, w1_words, w1_scales, offs
         half_offsets = [offsets[:, h * (HALF // 16) : (h + 1) * (HALF // 16)] for h in range(2)]
 
         rows = xT.rearrange("(p t) w -> p t w", t=PACK)
-        planes = [keep.tile([P, T], F32, name=f"plane{t}") for t in range(PACK)]
-        third, last = planes[2], planes[3]
+        planes = [keep.tile([P, T], F32, name=f"plane{t}") for t in range(2)]
+        last_two = keep.tile([P, 2 * T], F32, name="last_two")
+        third, last = last_two[:, 0:T], last_two[:, T : 2 * T]
         zp_cut = keep.tile([P, ZP_COLS], F32, name="zp_cut")
         nc.sync.dma_start(out=planes[0][:], in_=rows[:, 0, :])
         nc.sync.dma_start(offsets[:], offs)
         nc.sync.dma_start(out=zp_cut[:], in_=zp[0:1, :].rearrange("o (p c) -> (o p) c", c=ZP_COLS))
         nc.sync.dma_start(out=planes[1][:], in_=rows[:, 1, :])
-        nc.sync.dma_start(out=third[:], in_=rows[:, 2, :])
         chunks = []
         c0 = 0
         for width, scalar_share in LAST_CHUNKS:
             chunks.append((c0, c0 + scalar_share, c0 + width))
             c0 = c0 + width
-        for begin, middle, end in chunks:
-            nc.sync.dma_start(out=last[:, begin:end], in_=rows[:, 3, begin:end])
+        last_rows = rows[:, 2:4, :].rearrange("p t w -> p (t w)")
+        cuts = [0] + [T + end for begin, middle, end in chunks]
+        for begin, end in zip(cuts, cuts[1:]):
+            nc.sync.dma_start(out=last_two[:, begin:end], in_=last_rows[:, begin:end])
 
         w_codes = keep.tile([P, 2 * N], U8, name="w_codes", align_bytes=64)
         w_scales = keep.tile([P, N], U8, name="w_scales", align_bytes=64)
         csum_col = keep.tile([P, 1], F32, name="csum_col")
         nc.gpsimd.memset(w_scales[:].bitcast(I32), 0)
+        nc.sync.dma_start(out=csum_col[:], in_=csum)
+        csum_negated = keep.tile([P, 1], F32, name="csum_negated")
+        nc.gpsimd.tensor_scalar(csum_negated[:], csum_col[:], -1.0, 0.0, mybir.AluOpType.mult, mybir.AluOpType.add)
         nc.sync.dma_start(out=w_codes[:].bitcast(I32), in_=w1_words[0].bitcast(I32))
         for q in range(4):
             nc.sync.dma_start(
                 out=w_scales[32 * q : 32 * q + 4, :].bitcast(I32),
                 in_=w1_scales[0, 4 * q : 4 * q + 4, :].bitcast(I32),
             )
-        nc.sync.dma_start(out=csum_col[:], in_=csum)
 
         identity = keep.tile([P, P], F32, name="identity")
         make_identity(nc, identity[:])
@@ -85,22 +89,20 @@ def tile_picked_zeropt_none_l_kernel(tc, xT, zp, csum, w1_words, w1_scales, offs
 
         zp_picked = keep.tile([P, S], F32, name="zp_picked")
         nc.vector.tensor_copy(zp_picked[:], zp_table.indirect(offsets[:]))
-        zp_negated = keep.tile([P, S], F32, name="zp_negated")
-        nc.scalar.activation(zp_negated[:], zp_picked[:], COPY, scale=-1.0)
 
         picked = [keep.tile([P, HALF, PACK], BF16, name=f"picked{h}", align_bytes=64) for h in range(2)]
         picked_words = [picked[h][:].rearrange("p c t -> p (c t)").bitcast(U32).rearrange("p (c u) -> p c u", u=2) for h in range(2)]
 
-        nc.vector.tensor_copy(pairs[:, 1, HALF:S, 0], third[:].indirect(half_offsets[1]))
+        nc.vector.tensor_copy(pairs[:, 1, HALF:S, 0], third.indirect(half_offsets[1]))
         nc.scalar.copy(out=picked_words[1], in_=pair_words[:, HALF:S, :])
-        nc.vector.tensor_copy(pairs[:, 1, 0:HALF, 0], third[:].indirect(half_offsets[0]))
+        nc.vector.tensor_copy(pairs[:, 1, 0:HALF, 0], third.indirect(half_offsets[0]))
 
         last_bf16 = keep.tile([P, T], BF16, name="last_bf16")
         for begin, middle, end in chunks:
             nc.scalar.copy(out=last_bf16[:, begin:middle], in_=last[:, begin:middle])
             if middle < end:
                 nc.vector.tensor_copy(out=last_bf16[:, middle:end], in_=last[:, middle:end])
-        nc.vector.tensor_copy(pairs[:, 1, 0:HALF, 1], last[:].indirect(half_offsets[0]))
+        nc.vector.tensor_copy(pairs[:, 1, 0:HALF, 1], last.indirect(half_offsets[0]))
         picked_ints = picked[0][:].rearrange("p c t -> p (c t)").bitcast(I32).rearrange("p (c u) -> p c u", u=2)
         for first in range(0, HALF, PIECE):
             nc.vector.tensor_copy(out=picked_ints[:, first : first + PIECE, :], in_=pair_ints[:, first : first + PIECE, :])
@@ -136,5 +138,5 @@ def tile_picked_zeropt_none_l_kernel(tc, xT, zp, csum, w1_words, w1_scales, offs
             for first in range(0, PIECE, step):
                 part = slice(first, first + step)
                 cols = slice(i * PIECE + first, i * PIECE + first + step)
-                nc.vector.scalar_tensor_tensor(result[:, part], zp_negated[:, cols], csum_col[:, 0:1], sums[i][:, part], mybir.AluOpType.mult, mybir.AluOpType.add)
+                nc.vector.scalar_tensor_tensor(result[:, part], zp_picked[:, cols], csum_negated[:, 0:1], sums[i][:, part], mybir.AluOpType.mult, mybir.AluOpType.add)
                 nc.sync.dma_start(out=out[:, cols], in_=result[:, part])

@@ -22,7 +22,7 @@ HALF = S // 2
 ZP_COLS = T // P
 BANK_SLOTS = 4
 PIECE = 256
-LAST_CHUNKS = ((384, 384), (2560, 832), (896, 272), (256, 256))
+LAST_CHUNKS = ((576, 576), (2432, 768), (832, 256), (256, 256))
 
 
 def tile_picked_zeropt_none_l_kernel(tc, xT, zp, csum, w1_words, w1_scales, offs, out):

@@ -129,6 +129,8 @@ def tile_picked_zeropt_none_l_kernel(tc, xT, zp, csum, w1_words, w1_scales, offs
                 stop=True,
             )
             sums.append(y)
+        queues = (nc.sync, nc.scalar)
+        stores = 0
         for i in range(S // PIECE):
             if i < 2:
                 result = picked[1][:].rearrange("p c t -> p (c t)")[:, 2 * PIECE * i : 2 * PIECE * (i + 1)].bitcast(F32)
@@ -139,4 +141,5 @@ def tile_picked_zeropt_none_l_kernel(tc, xT, zp, csum, w1_words, w1_scales, offs
                 part = slice(first, first + step)
                 cols = slice(i * PIECE + first, i * PIECE + first + step)
                 nc.vector.scalar_tensor_tensor(result[:, part], zp_picked[:, cols], csum_negated[:, 0:1], sums[i][:, part], mybir.AluOpType.mult, mybir.AluOpType.add)
-                nc.sync.dma_start(out=out[:, cols], in_=result[:, part])
+                queues[stores % 2].dma_start(out=out[:, cols], in_=result[:, part])
+                stores = stores + 1

@@ -22,7 +22,7 @@ HALF = S // 2
 ZP_COLS = T // P
 BANK_SLOTS = 4
 PIECE = 256
-LAST_CHUNKS = ((576, 576), (2432, 768), (832, 256), (256, 256))
+LAST_CHUNKS = ((640, 640), (2368, 736), (832, 288), (256, 256))
 
 
 def tile_picked_zeropt_none_l_kernel(tc, xT, zp, csum, w1_words, w1_scales, offs, out):

@@ -15,14 +15,14 @@ U8 = mybir.dt.uint8
 FP8X4 = mybir.dt.float8_e4m3fn_x4
 FP4X4 = mybir.dt.float4_e2m1fn_x4
 COPY = mybir.ActivationFunctionType.Copy
+MULT = mybir.AluOpType.mult
+ADD = mybir.AluOpType.add
 
 P = 128
 PACK = 4
-HALF = S // 2
 ZP_COLS = T // P
 BANK_SLOTS = 4
 PIECE = 256
-LAST_CHUNKS = ((640, 640), (2368, 736), (832, 288), (256, 256))
 
 
 def tile_picked_zeropt_none_l_kernel(tc, xT, zp, csum, w1_words, w1_scales, offs, out):
@@ -33,90 +33,80 @@ def tile_picked_zeropt_none_l_kernel(tc, xT, zp, csum, w1_words, w1_scales, offs
         ybanks = ctx.enter_context(tc.psum_pool(name="ybanks", bufs=1))
 
         offsets = keep.tile([P, S // 16], U16, name="offsets")
-        half_offsets = [offsets[:, h * (HALF // 16) : (h + 1) * (HALF // 16)] for h in range(2)]
+
+        def entries(first, count):
+            return offsets[:, first // 16 : (first + count) // 16]
 
         rows = xT.rearrange("(p t) w -> p t w", t=PACK)
-        planes = [keep.tile([P, T], F32, name=f"plane{t}") for t in range(2)]
-        last_two = keep.tile([P, 2 * T], F32, name="last_two")
-        third, last = last_two[:, 0:T], last_two[:, T : 2 * T]
+        planes = [keep.tile([P, T], F32, name=f"plane{t}") for t in range(PACK)]
         zp_cut = keep.tile([P, ZP_COLS], F32, name="zp_cut")
         nc.sync.dma_start(out=planes[0][:], in_=rows[:, 0, :])
         nc.sync.dma_start(offsets[:], offs)
         nc.sync.dma_start(out=zp_cut[:], in_=zp[0:1, :].rearrange("o (p c) -> (o p) c", c=ZP_COLS))
-        nc.sync.dma_start(out=planes[1][:], in_=rows[:, 1, :])
-        chunks = []
-        c0 = 0
-        for width, scalar_share in LAST_CHUNKS:
-            chunks.append((c0, c0 + scalar_share, c0 + width))
-            c0 = c0 + width
-        last_rows = rows[:, 2:4, :].rearrange("p t w -> p (t w)")
-        cuts = [0] + [T + end for begin, middle, end in chunks]
-        for begin, end in zip(cuts, cuts[1:]):
-            nc.sync.dma_start(out=last_two[:, begin:end], in_=last_rows[:, begin:end])
+        for t in range(1, PACK):
+            nc.sync.dma_start(out=planes[t][:], in_=rows[:, t, :])
 
         w_codes = keep.tile([P, 2 * N], U8, name="w_codes", align_bytes=64)
         w_scales = keep.tile([P, N], U8, name="w_scales", align_bytes=64)
         csum_col = keep.tile([P, 1], F32, name="csum_col")
         nc.gpsimd.memset(w_scales[:].bitcast(I32), 0)
-        nc.sync.dma_start(out=csum_col[:], in_=csum)
-        csum_negated = keep.tile([P, 1], F32, name="csum_negated")
-        nc.gpsimd.tensor_scalar(csum_negated[:], csum_col[:], -1.0, 0.0, mybir.AluOpType.mult, mybir.AluOpType.add)
         nc.sync.dma_start(out=w_codes[:].bitcast(I32), in_=w1_words[0].bitcast(I32))
         for q in range(4):
             nc.sync.dma_start(
                 out=w_scales[32 * q : 32 * q + 4, :].bitcast(I32),
                 in_=w1_scales[0, 4 * q : 4 * q + 4, :].bitcast(I32),
             )
+        nc.sync.dma_start(out=csum_col[:], in_=csum)
 
         identity = keep.tile([P, P], F32, name="identity")
         make_identity(nc, identity[:])
 
-        space = keep.tile([P, S + T], F32, name="space")
-        zp_table = space[:, S : S + T]
-        pair_space = space[:, 0 : 2 * S]
-        pairs = pair_space.bitcast(BF16).rearrange("p (u c e) -> p u c e", u=2, e=2)
-        pair_words = pair_space.bitcast(U32).rearrange("p (u c) -> p c u", u=2)
-        pair_ints = pair_space.bitcast(I32).rearrange("p (u c) -> p c u", u=2)
-        for t in range(2):
-            nc.vector.tensor_copy(pairs[:, 0, :, t], planes[t][:].indirect(offsets[:]))
-        zp_runs = zp_table.rearrange("p (n a j) -> p a n j", a=ZP_COLS // BANK_SLOTS, j=BANK_SLOTS)
+        zp_table = keep.tile([P, T], F32, name="zp_table")
+        zp_runs = zp_table[:].rearrange("p (n a j) -> p a n j", a=ZP_COLS // BANK_SLOTS, j=BANK_SLOTS)
         for a in range(ZP_COLS // BANK_SLOTS):
             bank = zbanks.tile([P, BANK_SLOTS, P], F32, name="zbank")
             for j in range(BANK_SLOTS):
                 c = BANK_SLOTS * a + j
                 nc.tensor.transpose(bank[:, j, :], zp_cut[:, c : c + 1].to_broadcast([P, P]), identity[:])
             nc.scalar.copy(out=zp_runs[:, a, :, :], in_=bank[:].rearrange("p j n -> p n j"))
+        zp_negated = keep.tile([P, S], F32, name="zp_negated")
+        nc.scalar.activation(zp_negated[:], zp_table[:].indirect(offsets[:]), COPY, scale=-1.0)
 
-        zp_picked = keep.tile([P, S], F32, name="zp_picked")
-        nc.vector.tensor_copy(zp_picked[:], zp_table.indirect(offsets[:]))
+        pieces = S // PIECE
+        picked = [keep.tile([P, PIECE, PACK], BF16, name=f"picked{i}", align_bytes=64) for i in range(pieces)]
+        early = keep.tile([P, 2, S], BF16, name="early")
+        for t in range(2):
+            nc.vector.tensor_copy(early[:, t, :], planes[t][:].indirect(offsets[:]))
+        for i in range(pieces):
+            nc.vector.tensor_copy(out=picked[i][:, :, 0:2], in_=early[:, :, i * PIECE : (i + 1) * PIECE].rearrange("p t c -> p c t"))
 
-        picked = [keep.tile([P, HALF, PACK], BF16, name=f"picked{h}", align_bytes=64) for h in range(2)]
-        picked_words = [picked[h][:].rearrange("p c t -> p (c t)").bitcast(U32).rearrange("p (c u) -> p c u", u=2) for h in range(2)]
+        runs = [(0, 128), (128, 128), (256, 256), (512, 256), (768, 128), (896, 128)]
+        late = [keep.tile([P, 2, count], BF16, name=f"late{first}") for first, count in runs]
+        for r, (first, count) in enumerate(runs):
+            nc.vector.tensor_copy(late[r][:, 0, :], planes[2][:].indirect(entries(first, count)))
 
-        nc.vector.tensor_copy(pairs[:, 1, HALF:S, 0], third.indirect(half_offsets[1]))
-        nc.scalar.copy(out=picked_words[1], in_=pair_words[:, HALF:S, :])
-        nc.vector.tensor_copy(pairs[:, 1, 0:HALF, 0], third.indirect(half_offsets[0]))
+        def lay(copy, r):
+            first, count = runs[r]
+            i, at = divmod(first, PIECE)
+            copy(out=picked[i][:, at : at + count, 2:4], in_=late[r][:].rearrange("p t c -> p c t"))
 
-        last_bf16 = keep.tile([P, T], BF16, name="last_bf16")
-        for begin, middle, end in chunks:
-            nc.scalar.copy(out=last_bf16[:, begin:middle], in_=last[:, begin:middle])
-            if middle < end:
-                nc.vector.tensor_copy(out=last_bf16[:, middle:end], in_=last[:, middle:end])
-        nc.vector.tensor_copy(pairs[:, 1, 0:HALF, 1], last.indirect(half_offsets[0]))
-        picked_ints = picked[0][:].rearrange("p c t -> p (c t)").bitcast(I32).rearrange("p (c u) -> p c u", u=2)
-        for first in range(0, HALF, PIECE):
-            nc.vector.tensor_copy(out=picked_ints[:, first : first + PIECE, :], in_=pair_ints[:, first : first + PIECE, :])
-        nc.scalar.activation(picked[1][:, :, 3], last_bf16[:].indirect(half_offsets[1]), COPY)
+        for r in (0, 1):
+            nc.vector.tensor_copy(late[r][:, 1, :], planes[3][:].indirect(entries(*runs[r])))
+        for r in (2, 3, 4, 5):
+            nc.scalar.activation(late[r][:, 1, :], planes[3][:].indirect(entries(*runs[r])), COPY)
+        for r in (4, 5):
+            lay(nc.scalar.copy, r)
+        for r in (0, 1, 2, 3):
+            lay(nc.vector.tensor_copy, r)
 
         sums = []
-        for i in range(S // PIECE):
-            h, first = divmod(i * PIECE, HALF)
+        for i in range(pieces):
             x_codes = keep.tile([P, PIECE], U32, name=f"x_codes{i}", align_bytes=64)
             x_scales = keep.tile([P, PIECE], U8, name=f"x_scales{i}", align_bytes=64)
             nc.vector.quantize_mx(
                 out=x_codes[:].bitcast(FP8X4),
                 scales=x_scales[:],
-                in_=picked[h][:, first : first + PIECE, :].rearrange("p c t -> p (c t)"),
+                in_=picked[i][:].rearrange("p c t -> p (c t)"),
             )
             y = ybanks.tile([P, PIECE], F32, name=f"y{i}")
             nc.tensor.matmul_mx(
@@ -131,15 +121,15 @@ def tile_picked_zeropt_none_l_kernel(tc, xT, zp, csum, w1_words, w1_scales, offs
             sums.append(y)
         queues = (nc.sync, nc.scalar)
         stores = 0
-        for i in range(S // PIECE):
+        for i in range(pieces):
             if i < 2:
-                result = picked[1][:].rearrange("p c t -> p (c t)")[:, 2 * PIECE * i : 2 * PIECE * (i + 1)].bitcast(F32)
+                result = picked[2][:].rearrange("p c t -> p (c t)")[:, 2 * PIECE * i : 2 * PIECE * (i + 1)].bitcast(F32)
             else:
                 result = keep.tile([P, PIECE], F32, name=f"result{i}")[:]
             step = PIECE // 2 if i == 0 else PIECE
             for first in range(0, PIECE, step):
                 part = slice(first, first + step)
                 cols = slice(i * PIECE + first, i * PIECE + first + step)
-                nc.vector.scalar_tensor_tensor(result[:, part], zp_picked[:, cols], csum_negated[:, 0:1], sums[i][:, part], mybir.AluOpType.mult, mybir.AluOpType.add)
+                nc.vector.scalar_tensor_tensor(result[:, part], zp_negated[:, cols], csum_col[:, 0:1], sums[i][:, part], MULT, ADD)
                 queues[stores % 2].dma_start(out=out[:, cols], in_=result[:, part])
                 stores = stores + 1

@@ -22,14 +22,13 @@ P = 128
 PACK = 4
 ZP_COLS = T // P
 BANK_SLOTS = 4
-PIECE = 256
 
 
 def tile_picked_zeropt_none_l_kernel(tc, xT, zp, csum, w1_words, w1_scales, offs, out):
     nc = tc.nc
     with ExitStack() as ctx:
         keep = ctx.enter_context(tc.tile_pool(name="keep", bufs=1))
-        zbanks = ctx.enter_context(tc.psum_pool(name="zbanks", bufs=4))
+        zbanks = ctx.enter_context(tc.psum_pool(name="zbanks", bufs=3))
         ybanks = ctx.enter_context(tc.psum_pool(name="ybanks", bufs=1))
 
         offsets = keep.tile([P, S // 16], U16, name="offsets")
@@ -50,13 +49,13 @@ def tile_picked_zeropt_none_l_kernel(tc, xT, zp, csum, w1_words, w1_scales, offs
         w_scales = keep.tile([P, N], U8, name="w_scales", align_bytes=64)
         csum_col = keep.tile([P, 1], F32, name="csum_col")
         nc.gpsimd.memset(w_scales[:].bitcast(I32), 0)
+        nc.sync.dma_start(out=csum_col[:], in_=csum)
         nc.sync.dma_start(out=w_codes[:].bitcast(I32), in_=w1_words[0].bitcast(I32))
         for q in range(4):
             nc.sync.dma_start(
                 out=w_scales[32 * q : 32 * q + 4, :].bitcast(I32),
                 in_=w1_scales[0, 4 * q : 4 * q + 4, :].bitcast(I32),
             )
-        nc.sync.dma_start(out=csum_col[:], in_=csum)
 
         identity = keep.tile([P, P], F32, name="identity")
         make_identity(nc, identity[:])
@@ -72,45 +71,39 @@ def tile_picked_zeropt_none_l_kernel(tc, xT, zp, csum, w1_words, w1_scales, offs
         zp_negated = keep.tile([P, S], F32, name="zp_negated")
         nc.scalar.activation(zp_negated[:], zp_table[:].indirect(offsets[:]), COPY, scale=-1.0)
 
-        pieces = S // PIECE
-        picked = [keep.tile([P, PIECE, PACK], BF16, name=f"picked{i}", align_bytes=64) for i in range(pieces)]
+        runs = [(0, 128), (128, 128), (256, 256), (512, 256), (768, 128), (896, 128)]
+        pieces = [(0, 256), (256, 256), (512, 256), (768, 128), (896, 128)]
+        picked = [keep.tile([P, count, PACK], BF16, name=f"picked{first}", align_bytes=64) for first, count in pieces]
         early = keep.tile([P, 2, S], BF16, name="early")
         for t in range(2):
             nc.vector.tensor_copy(early[:, t, :], planes[t][:].indirect(offsets[:]))
-        for i in range(pieces):
-            nc.vector.tensor_copy(out=picked[i][:, :, 0:2], in_=early[:, :, i * PIECE : (i + 1) * PIECE].rearrange("p t c -> p c t"))
+        for i, (first, count) in enumerate(pieces):
+            nc.vector.tensor_copy(out=picked[i][:, :, 0:2], in_=early[:, :, first : first + count].rearrange("p t c -> p c t"))
 
-        runs = [(0, 128), (128, 128), (256, 256), (512, 256), (768, 128), (896, 128)]
         late = [keep.tile([P, 2, count], BF16, name=f"late{first}") for first, count in runs]
         for r, (first, count) in enumerate(runs):
             nc.vector.tensor_copy(late[r][:, 0, :], planes[2][:].indirect(entries(first, count)))
 
         def lay(copy, r):
             first, count = runs[r]
-            i, at = divmod(first, PIECE)
+            i = max(j for j, piece in enumerate(pieces) if piece[0] <= first)
+            at = first - pieces[i][0]
             copy(out=picked[i][:, at : at + count, 2:4], in_=late[r][:].rearrange("p t c -> p c t"))
 
-        for r in (0, 1):
-            nc.vector.tensor_copy(late[r][:, 1, :], planes[3][:].indirect(entries(*runs[r])))
-        for r in (2, 3, 4, 5):
-            nc.scalar.activation(late[r][:, 1, :], planes[3][:].indirect(entries(*runs[r])), COPY)
-        for r in (4, 5):
-            lay(nc.scalar.copy, r)
-        for r in (0, 1, 2, 3):
-            lay(nc.vector.tensor_copy, r)
+        sums = {}
 
-        sums = []
-        for i in range(pieces):
-            x_codes = keep.tile([P, PIECE], U32, name=f"x_codes{i}", align_bytes=64)
-            x_scales = keep.tile([P, PIECE], U8, name=f"x_scales{i}", align_bytes=64)
+        def multiply(i):
+            first, count = pieces[i]
+            x_codes = keep.tile([P, count], U32, name=f"x_codes{first}", align_bytes=64)
+            x_scales = keep.tile([P, count], U8, name=f"x_scales{first}", align_bytes=64)
             nc.vector.quantize_mx(
                 out=x_codes[:].bitcast(FP8X4),
                 scales=x_scales[:],
                 in_=picked[i][:].rearrange("p c t -> p (c t)"),
             )
-            y = ybanks.tile([P, PIECE], F32, name=f"y{i}")
+            sums[i] = ybanks.tile([P, count], F32, name=f"y{first}")
             nc.tensor.matmul_mx(
-                out=y[:],
+                out=sums[i][:],
                 lhsT=w_codes[:].bitcast(FP4X4),
                 lhsT_scale=w_scales[:],
                 rhs=x_codes[:].bitcast(FP8X4),
@@ -118,18 +111,30 @@ def tile_picked_zeropt_none_l_kernel(tc, xT, zp, csum, w1_words, w1_scales, offs
                 start=True,
                 stop=True,
             )
-            sums.append(y)
+
         queues = (nc.sync, nc.scalar)
-        stores = 0
-        for i in range(pieces):
-            if i < 2:
-                result = picked[2][:].rearrange("p c t -> p (c t)")[:, 2 * PIECE * i : 2 * PIECE * (i + 1)].bitcast(F32)
-            else:
-                result = keep.tile([P, PIECE], F32, name=f"result{i}")[:]
-            step = PIECE // 2 if i == 0 else PIECE
-            for first in range(0, PIECE, step):
-                part = slice(first, first + step)
-                cols = slice(i * PIECE + first, i * PIECE + first + step)
-                nc.vector.scalar_tensor_tensor(result[:, part], zp_negated[:, cols], csum_col[:, 0:1], sums[i][:, part], MULT, ADD)
-                queues[stores % 2].dma_start(out=out[:, cols], in_=result[:, part])
-                stores = stores + 1
+
+        def correct(i):
+            first, count = pieces[i]
+            cols = slice(first, first + count)
+            result = keep.tile([P, count], F32, name=f"result{first}")
+            nc.vector.scalar_tensor_tensor(result[:], zp_negated[:, cols], csum_col[:, 0:1], sums[i][:], MULT, ADD)
+            queues[i % 2].dma_start(out=out[:, cols], in_=result[:])
+
+        for r in (0, 1):
+            nc.vector.tensor_copy(late[r][:, 1, :], planes[3][:].indirect(entries(*runs[r])))
+        for r in (2, 3, 4, 5):
+            nc.scalar.activation(late[r][:, 1, :], planes[3][:].indirect(entries(*runs[r])), COPY)
+        for r in (4, 5):
+            lay(nc.scalar.copy, r)
+        for r in (0, 1, 2):
+            lay(nc.vector.tensor_copy, r)
+        multiply(0)
+        lay(nc.vector.tensor_copy, 3)
+        multiply(1)
+        multiply(2)
+        correct(0)
+        multiply(3)
+        multiply(4)
+        for i in range(1, len(pieces)):
+            correct(i)

@@ -22,6 +22,7 @@ P = 128
 PACK = 4
 ZP_COLS = T // P
 BANK_SLOTS = 4
+STORE = 256
 
 
 def tile_picked_zeropt_none_l_kernel(tc, xT, zp, csum, w1_words, w1_scales, offs, out):
@@ -71,7 +72,7 @@ def tile_picked_zeropt_none_l_kernel(tc, xT, zp, csum, w1_words, w1_scales, offs
         zp_negated = keep.tile([P, S], F32, name="zp_negated")
         nc.scalar.activation(zp_negated[:], zp_table[:].indirect(offsets[:]), COPY, scale=-1.0)
 
-        runs = [(0, 128), (128, 128), (256, 256), (512, 256), (768, 128), (896, 128)]
+        runs = [(0, 128), (128, 128), (256, 256), (512, 192), (704, 192), (896, 128)]
         pieces = [(0, 256), (256, 256), (512, 256), (768, 128), (896, 128)]
         picked = [keep.tile([P, count, PACK], BF16, name=f"picked{first}", align_bytes=64) for first, count in pieces]
         early = keep.tile([P, 2, S], BF16, name="early")
@@ -84,20 +85,27 @@ def tile_picked_zeropt_none_l_kernel(tc, xT, zp, csum, w1_words, w1_scales, offs
         for r, (first, count) in enumerate(runs):
             nc.vector.tensor_copy(late[r][:, 0, :], planes[2][:].indirect(entries(first, count)))
 
+        def fetch_on_vector(r):
+            nc.vector.tensor_copy(late[r][:, 1, :], planes[3][:].indirect(entries(*runs[r])))
+
+        def fetch_on_scalar(r):
+            nc.scalar.activation(late[r][:, 1, :], planes[3][:].indirect(entries(*runs[r])), COPY)
+
         def lay(copy, r):
             first, count = runs[r]
-            i = max(j for j, piece in enumerate(pieces) if piece[0] <= first)
-            at = first - pieces[i][0]
-            copy(out=picked[i][:, at : at + count, 2:4], in_=late[r][:].rearrange("p t c -> p c t"))
+            for i, (begin, width) in enumerate(pieces):
+                low, high = max(first, begin), min(first + count, begin + width)
+                if low < high:
+                    copy(out=picked[i][:, low - begin : high - begin, 2:4], in_=late[r][:, :, low - first : high - first].rearrange("p t c -> p c t"))
 
+        codes = [keep.tile([P, 256], U32, name=f"x_codes{j}", align_bytes=64) for j in range(3)]
         sums = {}
 
-        def multiply(i):
+        def multiply(i, x_codes):
             first, count = pieces[i]
-            x_codes = keep.tile([P, count], U32, name=f"x_codes{first}", align_bytes=64)
             x_scales = keep.tile([P, count], U8, name=f"x_scales{first}", align_bytes=64)
             nc.vector.quantize_mx(
-                out=x_codes[:].bitcast(FP8X4),
+                out=x_codes.bitcast(FP8X4),
                 scales=x_scales[:],
                 in_=picked[i][:].rearrange("p c t -> p (c t)"),
             )
@@ -106,7 +114,7 @@ def tile_picked_zeropt_none_l_kernel(tc, xT, zp, csum, w1_words, w1_scales, offs
                 out=sums[i][:],
                 lhsT=w_codes[:].bitcast(FP4X4),
                 lhsT_scale=w_scales[:],
-                rhs=x_codes[:].bitcast(FP8X4),
+                rhs=x_codes.bitcast(FP8X4),
                 rhs_scale=x_scales[:],
                 start=True,
                 stop=True,
@@ -114,27 +122,29 @@ def tile_picked_zeropt_none_l_kernel(tc, xT, zp, csum, w1_words, w1_scales, offs
 
         queues = (nc.sync, nc.scalar)
 
+        results = [keep.tile([P, STORE], F32, name=f"result{j}") for j in range(S // STORE)]
+
         def correct(i):
             first, count = pieces[i]
-            cols = slice(first, first + count)
-            result = keep.tile([P, count], F32, name=f"result{first}")
-            nc.vector.scalar_tensor_tensor(result[:], zp_negated[:, cols], csum_col[:, 0:1], sums[i][:], MULT, ADD)
-            queues[i % 2].dma_start(out=out[:, cols], in_=result[:])
+            j, at = divmod(first, STORE)
+            nc.vector.scalar_tensor_tensor(results[j][:, at : at + count], zp_negated[:, first : first + count], csum_col[:, 0:1], sums[i][:], MULT, ADD)
+            if at + count == STORE:
+                queues[(j + 1) % 2].dma_start(out=out[:, j * STORE : (j + 1) * STORE], in_=results[j][:])
 
         for r in (0, 1):
-            nc.vector.tensor_copy(late[r][:, 1, :], planes[3][:].indirect(entries(*runs[r])))
+            fetch_on_vector(r)
         for r in (2, 3, 4, 5):
-            nc.scalar.activation(late[r][:, 1, :], planes[3][:].indirect(entries(*runs[r])), COPY)
-        for r in (4, 5):
-            lay(nc.scalar.copy, r)
+            fetch_on_scalar(r)
+        lay(nc.scalar.copy, 4)
+        lay(nc.scalar.copy, 5)
         for r in (0, 1, 2):
             lay(nc.vector.tensor_copy, r)
-        multiply(0)
+        multiply(0, codes[0][:])
         lay(nc.vector.tensor_copy, 3)
-        multiply(1)
-        multiply(2)
+        multiply(1, codes[1][:])
+        multiply(2, codes[2][:])
         correct(0)
-        multiply(3)
-        multiply(4)
+        multiply(3, codes[0][:, 0:128])
+        multiply(4, codes[0][:, 128:256])
         for i in range(1, len(pieces)):
             correct(i)

@@ -23,13 +23,16 @@ PACK = 4
 ZP_COLS = T // P
 BANK_SLOTS = 4
 STORE = 256
+RUN = 128
+OWN = 512
+LAST = 256
 
 
 def tile_picked_zeropt_none_l_kernel(tc, xT, zp, csum, w1_words, w1_scales, offs, out):
     nc = tc.nc
     with ExitStack() as ctx:
         keep = ctx.enter_context(tc.tile_pool(name="keep", bufs=1))
-        zbanks = ctx.enter_context(tc.psum_pool(name="zbanks", bufs=3))
+        zbanks = ctx.enter_context(tc.psum_pool(name="zbanks", bufs=4))
         ybanks = ctx.enter_context(tc.psum_pool(name="ybanks", bufs=1))
 
         offsets = keep.tile([P, S // 16], U16, name="offsets")
@@ -72,46 +75,56 @@ def tile_picked_zeropt_none_l_kernel(tc, xT, zp, csum, w1_words, w1_scales, offs
         zp_negated = keep.tile([P, S], F32, name="zp_negated")
         nc.scalar.activation(zp_negated[:], zp_table[:].indirect(offsets[:]), COPY, scale=-1.0)
 
-        runs = [(0, 128), (128, 128), (256, 256), (512, 192), (704, 192), (896, 128)]
-        pieces = [(0, 256), (256, 256), (512, 256), (768, 128), (896, 128)]
-        picked = [keep.tile([P, count, PACK], BF16, name=f"picked{first}", align_bytes=64) for first, count in pieces]
+        picked_own = keep.tile([P, OWN, PACK], BF16, name="picked_own", align_bytes=64)
+        runs = range((S - OWN) // RUN)
+        picked = [keep.tile([P, RUN, PACK], BF16, name=f"picked{r}", align_bytes=64) for r in runs]
         early = keep.tile([P, 2, S], BF16, name="early")
         for t in range(2):
             nc.vector.tensor_copy(early[:, t, :], planes[t][:].indirect(offsets[:]))
-        for i, (first, count) in enumerate(pieces):
-            nc.vector.tensor_copy(out=picked[i][:, :, 0:2], in_=early[:, :, first : first + count].rearrange("p t c -> p c t"))
+        nc.vector.tensor_copy(out=picked_own[:, :, 0:2], in_=early[:, :, S - OWN - LAST : S - LAST].rearrange("p t c -> p c t"))
 
-        late = [keep.tile([P, 2, count], BF16, name=f"late{first}") for first, count in runs]
-        for r, (first, count) in enumerate(runs):
-            nc.vector.tensor_copy(late[r][:, 0, :], planes[2][:].indirect(entries(first, count)))
+        def first_of(r):
+            return r * RUN if r * RUN < S - OWN - LAST else OWN + r * RUN
 
-        def fetch_on_vector(r):
-            nc.vector.tensor_copy(late[r][:, 1, :], planes[3][:].indirect(entries(*runs[r])))
+        own_first = S - OWN - LAST
+        late = []
+        for r in runs:
+            nc.vector.tensor_copy(out=picked[r][:, :, 0:2], in_=early[:, :, first_of(r) : first_of(r) + RUN].rearrange("p t c -> p c t"))
+            late.append(keep.tile([P, 2 if r < 2 else 1, RUN], BF16, name=f"late{r}", tag=f"late{r}", align_bytes=64))
+            nc.vector.tensor_copy(late[r][:, 0, :], planes[2][:].indirect(entries(first_of(r), RUN)))
+            if r >= 2:
+                nc.scalar.copy(out=picked[r][:, :, 2], in_=late[r][:, 0, :])
+        for t in (2, 3):
+            nc.vector.tensor_copy(picked_own[:, :, t], planes[t][:].indirect(entries(own_first, OWN)))
 
-        def fetch_on_scalar(r):
-            nc.scalar.activation(late[r][:, 1, :], planes[3][:].indirect(entries(*runs[r])), COPY)
+        def fetch(r):
+            nc.scalar.activation(late[r][:, 1, :], planes[3][:].indirect(entries(first_of(r), RUN)), COPY)
 
-        def lay(copy, r):
-            first, count = runs[r]
-            for i, (begin, width) in enumerate(pieces):
-                low, high = max(first, begin), min(first + count, begin + width)
-                if low < high:
-                    copy(out=picked[i][:, low - begin : high - begin, 2:4], in_=late[r][:, :, low - first : high - first].rearrange("p t c -> p c t"))
+        def lay(r):
+            nc.scalar.copy(out=picked[r][:, :, 2:4], in_=late[r][:].rearrange("p t c -> p c t"))
 
-        codes = [keep.tile([P, 256], U32, name=f"x_codes{j}", align_bytes=64) for j in range(3)]
+        for r in (0, 1):
+            fetch(r)
+        for r in (0, 1):
+            lay(r)
+        last = keep.tile([P, 2, RUN], BF16, name="last", tag="late0", align_bytes=64)
+        for r in (2, 3):
+            nc.scalar.activation(last[:, r - 2, :], planes[3][:].indirect(entries(first_of(r), RUN)), COPY)
+        for r in (2, 3):
+            nc.scalar.copy(out=picked[r][:, :, 3], in_=last[:, r - 2, :])
+
         sums = {}
 
-        def multiply(i, x_codes):
-            first, count = pieces[i]
+        def multiply(first, count, source, x_codes, y):
             x_scales = keep.tile([P, count], U8, name=f"x_scales{first}", align_bytes=64)
             nc.vector.quantize_mx(
                 out=x_codes.bitcast(FP8X4),
                 scales=x_scales[:],
-                in_=picked[i][:].rearrange("p c t -> p (c t)"),
+                in_=source.rearrange("p c t -> p (c t)"),
             )
-            sums[i] = ybanks.tile([P, count], F32, name=f"y{first}")
+            sums[first] = y
             nc.tensor.matmul_mx(
-                out=sums[i][:],
+                out=y,
                 lhsT=w_codes[:].bitcast(FP4X4),
                 lhsT_scale=w_scales[:],
                 rhs=x_codes.bitcast(FP8X4),
@@ -121,30 +134,25 @@ def tile_picked_zeropt_none_l_kernel(tc, xT, zp, csum, w1_words, w1_scales, offs
             )
 
         queues = (nc.sync, nc.scalar)
-
         results = [keep.tile([P, STORE], F32, name=f"result{j}") for j in range(S // STORE)]
 
-        def correct(i):
-            first, count = pieces[i]
+        def correct(first, count):
             j, at = divmod(first, STORE)
-            nc.vector.scalar_tensor_tensor(results[j][:, at : at + count], zp_negated[:, first : first + count], csum_col[:, 0:1], sums[i][:], MULT, ADD)
+            nc.vector.scalar_tensor_tensor(results[j][:, at : at + count], zp_negated[:, first : first + count], csum_col[:, 0:1], sums[first], MULT, ADD)
             if at + count == STORE:
                 queues[(j + 1) % 2].dma_start(out=out[:, j * STORE : (j + 1) * STORE], in_=results[j][:])
 
+        run_codes = [keep.tile([P, RUN], U32, name=f"run_codes{r}", align_bytes=64) for r in range(3)]
         for r in (0, 1):
-            fetch_on_vector(r)
-        for r in (2, 3, 4, 5):
-            fetch_on_scalar(r)
-        lay(nc.scalar.copy, 4)
-        lay(nc.scalar.copy, 5)
-        for r in (0, 1, 2):
-            lay(nc.vector.tensor_copy, r)
-        multiply(0, codes[0][:])
-        lay(nc.vector.tensor_copy, 3)
-        multiply(1, codes[1][:])
-        multiply(2, codes[2][:])
-        correct(0)
-        multiply(3, codes[0][:, 0:128])
-        multiply(4, codes[0][:, 128:256])
-        for i in range(1, len(pieces)):
-            correct(i)
+            multiply(first_of(r), RUN, picked[r][:], run_codes[r][:], ybanks.tile([P, RUN], F32, name=f"y_run{r}")[:])
+        own_codes = keep.tile([P, OWN], U32, name="own_codes", tag="late1", align_bytes=64)
+        for h in range(2):
+            multiply(own_first + h * STORE, STORE, picked_own[:, h * STORE : (h + 1) * STORE, :], own_codes[:, h * STORE : (h + 1) * STORE], ybanks.tile([P, STORE], F32, name=f"y_own{h}")[:])
+        multiply(first_of(2), RUN, picked[2][:], run_codes[2][:], zbanks.tile([P, BANK_SLOTS, P], F32, name="zbank")[:, 0, :])
+        for r in (0, 1):
+            correct(first_of(r), RUN)
+        multiply(first_of(3), RUN, picked[3][:], run_codes[1][:], zbanks.tile([P, BANK_SLOTS, P], F32, name="zbank")[:, 0, :])
+        for h in range(2):
+            correct(own_first + h * STORE, STORE)
+        for r in (2, 3):
+            correct(first_of(r), RUN)

@@ -90,10 +90,8 @@ def tile_picked_zeropt_none_l_kernel(tc, xT, zp, csum, w1_words, w1_scales, offs
         late = []
         for r in runs:
             nc.vector.tensor_copy(out=picked[r][:, :, 0:2], in_=early[:, :, first_of(r) : first_of(r) + RUN].rearrange("p t c -> p c t"))
-            late.append(keep.tile([P, 2 if r < 2 else 1, RUN], BF16, name=f"late{r}", tag=f"late{r}", align_bytes=64))
+            late.append(keep.tile([P, 2, RUN], BF16, name=f"late{r}", tag=f"late{r}", align_bytes=64))
             nc.vector.tensor_copy(late[r][:, 0, :], planes[2][:].indirect(entries(first_of(r), RUN)))
-            if r >= 2:
-                nc.scalar.copy(out=picked[r][:, :, 2], in_=late[r][:, 0, :])
         for t in (2, 3):
             nc.vector.tensor_copy(picked_own[:, :, t], planes[t][:].indirect(entries(own_first, OWN)))
 
@@ -103,15 +101,12 @@ def tile_picked_zeropt_none_l_kernel(tc, xT, zp, csum, w1_words, w1_scales, offs
         def lay(r):
             nc.scalar.copy(out=picked[r][:, :, 2:4], in_=late[r][:].rearrange("p t c -> p c t"))
 
-        for r in (0, 1):
+        for r in runs:
             fetch(r)
         for r in (0, 1):
+            nc.gpsimd.tensor_scalar(picked[r][:, :, 2:4], late[r][:].rearrange("p t c -> p c t"), 1.0, 0.0, MULT, ADD)
+        for r in (2, 3):
             lay(r)
-        last = keep.tile([P, 2, RUN], BF16, name="last", tag="late0", align_bytes=64)
-        for r in (2, 3):
-            nc.scalar.activation(last[:, r - 2, :], planes[3][:].indirect(entries(first_of(r), RUN)), COPY)
-        for r in (2, 3):
-            nc.scalar.copy(out=picked[r][:, :, 3], in_=last[:, r - 2, :])
 
         sums = {}
 
@@ -133,14 +128,13 @@ def tile_picked_zeropt_none_l_kernel(tc, xT, zp, csum, w1_words, w1_scales, offs
                 stop=True,
             )
 
-        queues = (nc.sync, nc.scalar)
         results = [keep.tile([P, STORE], F32, name=f"result{j}") for j in range(S // STORE)]
 
         def correct(first, count):
             j, at = divmod(first, STORE)
             nc.vector.scalar_tensor_tensor(results[j][:, at : at + count], zp_negated[:, first : first + count], csum_col[:, 0:1], sums[first], MULT, ADD)
             if at + count == STORE:
-                queues[(j + 1) % 2].dma_start(out=out[:, j * STORE : (j + 1) * STORE], in_=results[j][:])
+                nc.sync.dma_start(out=out[:, j * STORE : (j + 1) * STORE], in_=results[j][:])
 
         run_codes = [keep.tile([P, RUN], U32, name=f"run_codes{r}", align_bytes=64) for r in range(3)]
         for r in (0, 1):

@@ -103,8 +103,10 @@ def tile_picked_zeropt_none_l_kernel(tc, xT, zp, csum, w1_words, w1_scales, offs
 
         for r in runs:
             fetch(r)
-        for r in (0, 1):
-            nc.gpsimd.tensor_scalar(picked[r][:, :, 2:4], late[r][:].rearrange("p t c -> p c t"), 1.0, 0.0, MULT, ADD)
+        half = RUN // 2
+        for r, count in ((0, RUN), (1, half)):
+            nc.gpsimd.tensor_scalar(picked[r][:, :count, 2:4], late[r][:, :, :count].rearrange("p t c -> p c t"), 1.0, 0.0, MULT, ADD)
+        nc.scalar.copy(out=picked[1][:, half:, 2:4], in_=late[1][:, :, half:].rearrange("p t c -> p c t"))
         for r in (2, 3):
             lay(r)
 
@@ -137,14 +139,15 @@ def tile_picked_zeropt_none_l_kernel(tc, xT, zp, csum, w1_words, w1_scales, offs
                 nc.sync.dma_start(out=out[:, j * STORE : (j + 1) * STORE], in_=results[j][:])
 
         run_codes = [keep.tile([P, RUN], U32, name=f"run_codes{r}", align_bytes=64) for r in range(3)]
+        y_first = ybanks.tile([P, STORE], F32, name="y_first")
         for r in (0, 1):
-            multiply(first_of(r), RUN, picked[r][:], run_codes[r][:], ybanks.tile([P, RUN], F32, name=f"y_run{r}")[:])
+            multiply(first_of(r), RUN, picked[r][:], run_codes[r][:], y_first[:, r * RUN : (r + 1) * RUN])
+        sums[0] = y_first[:]
         own_codes = keep.tile([P, OWN], U32, name="own_codes", tag="late1", align_bytes=64)
         for h in range(2):
             multiply(own_first + h * STORE, STORE, picked_own[:, h * STORE : (h + 1) * STORE, :], own_codes[:, h * STORE : (h + 1) * STORE], ybanks.tile([P, STORE], F32, name=f"y_own{h}")[:])
         multiply(first_of(2), RUN, picked[2][:], run_codes[2][:], zbanks.tile([P, BANK_SLOTS, P], F32, name="zbank")[:, 0, :])
-        for r in (0, 1):
-            correct(first_of(r), RUN)
+        correct(0, STORE)
         multiply(first_of(3), RUN, picked[3][:], run_codes[1][:], zbanks.tile([P, BANK_SLOTS, P], F32, name="zbank")[:, 0, :])
         for h in range(2):
             correct(own_first + h * STORE, STORE)

@@ -87,10 +87,12 @@ def tile_picked_zeropt_none_l_kernel(tc, xT, zp, csum, w1_words, w1_scales, offs
             return r * RUN if r * RUN < S - OWN - LAST else OWN + r * RUN
 
         own_first = S - OWN - LAST
-        late = []
+        shared = keep.tile([P, 3, RUN], BF16, name="late_shared", align_bytes=64)
+        late1 = keep.tile([P, 2, RUN], BF16, name="late1", tag="late1", align_bytes=64)
+        late2 = keep.tile([P, 2, RUN], BF16, name="late2", align_bytes=64)
+        late = (shared[:, 1:3, :], late1[:], late2[:], shared[:, 0:2, :])
         for r in runs:
             nc.vector.tensor_copy(out=picked[r][:, :, 0:2], in_=early[:, :, first_of(r) : first_of(r) + RUN].rearrange("p t c -> p c t"))
-            late.append(keep.tile([P, 2, RUN], BF16, name=f"late{r}", tag=f"late{r}", align_bytes=64))
             nc.vector.tensor_copy(late[r][:, 0, :], planes[2][:].indirect(entries(first_of(r), RUN)))
         for t in (2, 3):
             nc.vector.tensor_copy(picked_own[:, :, t], planes[t][:].indirect(entries(own_first, OWN)))
@@ -99,14 +101,13 @@ def tile_picked_zeropt_none_l_kernel(tc, xT, zp, csum, w1_words, w1_scales, offs
             nc.scalar.activation(late[r][:, 1, :], planes[3][:].indirect(entries(first_of(r), RUN)), COPY)
 
         def lay(r):
-            nc.scalar.copy(out=picked[r][:, :, 2:4], in_=late[r][:].rearrange("p t c -> p c t"))
+            nc.scalar.copy(out=picked[r][:, :, 2:4], in_=late[r].rearrange("p t c -> p c t"))
 
-        for r in runs:
+        for r in range(3):
             fetch(r)
-        half = RUN // 2
-        for r, count in ((0, RUN), (1, half)):
-            nc.gpsimd.tensor_scalar(picked[r][:, :count, 2:4], late[r][:, :, :count].rearrange("p t c -> p c t"), 1.0, 0.0, MULT, ADD)
-        nc.scalar.copy(out=picked[1][:, half:, 2:4], in_=late[1][:, :, half:].rearrange("p t c -> p c t"))
+        nc.gpsimd.tensor_scalar(picked[0][:, :, 2:4], late[0].rearrange("p t c -> p c t"), 1.0, 0.0, MULT, ADD)
+        lay(1)
+        fetch(3)
         for r in (2, 3):
             lay(r)
 

@@ -51,15 +51,16 @@ def tile_picked_zeropt_none_l_kernel(tc, xT, zp, csum, w1_words, w1_scales, offs
 
         w_codes = keep.tile([P, 2 * N], U8, name="w_codes", align_bytes=64)
         w_scales = keep.tile([P, N], U8, name="w_scales", align_bytes=64)
-        csum_col = keep.tile([P, 1], F32, name="csum_col")
+        csum_col = keep.tile([P, 1], F32, name="csum_col", tag="csum", align_bytes=64)
         nc.gpsimd.memset(w_scales[:].bitcast(I32), 0)
-        nc.sync.dma_start(out=csum_col[:], in_=csum)
         nc.sync.dma_start(out=w_codes[:].bitcast(I32), in_=w1_words[0].bitcast(I32))
         for q in range(4):
             nc.sync.dma_start(
                 out=w_scales[32 * q : 32 * q + 4, :].bitcast(I32),
                 in_=w1_scales[0, 4 * q : 4 * q + 4, :].bitcast(I32),
             )
+
+        nc.sync.dma_start(out=csum_col[:], in_=csum)
 
         identity = keep.tile([P, P], F32, name="identity")
         make_identity(nc, identity[:])
@@ -72,8 +73,8 @@ def tile_picked_zeropt_none_l_kernel(tc, xT, zp, csum, w1_words, w1_scales, offs
                 c = BANK_SLOTS * a + j
                 nc.tensor.transpose(bank[:, j, :], zp_cut[:, c : c + 1].to_broadcast([P, P]), identity[:])
             nc.scalar.copy(out=zp_runs[:, a, :, :], in_=bank[:].rearrange("p j n -> p n j"))
-        zp_negated = keep.tile([P, S], F32, name="zp_negated")
-        nc.scalar.activation(zp_negated[:], zp_table[:].indirect(offsets[:]), COPY, scale=-1.0)
+        zp_picked = keep.tile([P, S], F32, name="zp_picked")
+        nc.scalar.activation(zp_picked[:], zp_table[:].indirect(offsets[:]), COPY)
 
         picked_own = keep.tile([P, OWN, PACK], BF16, name="picked_own", align_bytes=64)
         runs = range((S - OWN) // RUN)
@@ -106,6 +107,8 @@ def tile_picked_zeropt_none_l_kernel(tc, xT, zp, csum, w1_words, w1_scales, offs
         for r in range(3):
             fetch(r)
         nc.gpsimd.tensor_scalar(picked[0][:, :, 2:4], late[0].rearrange("p t c -> p c t"), 1.0, 0.0, MULT, ADD)
+        csum_negated = keep.tile([P, 1], F32, name="csum_negated")
+        nc.gpsimd.tensor_scalar(csum_negated[:], csum_col[:], -1.0, 0.0, MULT, ADD)
         lay(1)
         fetch(3)
         for r in (2, 3):
@@ -114,7 +117,8 @@ def tile_picked_zeropt_none_l_kernel(tc, xT, zp, csum, w1_words, w1_scales, offs
         sums = {}
 
         def multiply(first, count, source, x_codes, y):
-            x_scales = keep.tile([P, count], U8, name=f"x_scales{first}", align_bytes=64)
+            tag = "csum" if first == S - RUN else f"x_scales{first}"
+            x_scales = keep.tile([P, count], U8, name=f"x_scales{first}", tag=tag, align_bytes=64)
             nc.vector.quantize_mx(
                 out=x_codes.bitcast(FP8X4),
                 scales=x_scales[:],
@@ -135,7 +139,7 @@ def tile_picked_zeropt_none_l_kernel(tc, xT, zp, csum, w1_words, w1_scales, offs
 
         def correct(first, count):
             j, at = divmod(first, STORE)
-            nc.vector.scalar_tensor_tensor(results[j][:, at : at + count], zp_negated[:, first : first + count], csum_col[:, 0:1], sums[first], MULT, ADD)
+            nc.vector.scalar_tensor_tensor(results[j][:, at : at + count], zp_picked[:, first : first + count], csum_negated[:, 0:1], sums[first], MULT, ADD)
             if at + count == STORE:
                 nc.sync.dma_start(out=out[:, j * STORE : (j + 1) * STORE], in_=results[j][:])
 

@@ -25,7 +25,6 @@ BANK_SLOTS = 4
 STORE = 256
 RUN = 128
 OWN = 512
-LAST = 256
 
 
 def tile_picked_zeropt_none_l_kernel(tc, xT, zp, csum, w1_words, w1_scales, offs, out):
@@ -41,13 +40,15 @@ def tile_picked_zeropt_none_l_kernel(tc, xT, zp, csum, w1_words, w1_scales, offs
             return offsets[:, first // 16 : (first + count) // 16]
 
         rows = xT.rearrange("(p t) w -> p t w", t=PACK)
-        planes = [keep.tile([P, T], F32, name=f"plane{t}") for t in range(PACK)]
+        middle = keep.tile([P, 2, T], F32, name="middle")
+        planes = {t: keep.tile([P, T], F32, name=f"plane{t}") for t in (0, 3)}
         zp_cut = keep.tile([P, ZP_COLS], F32, name="zp_cut")
         nc.sync.dma_start(out=planes[0][:], in_=rows[:, 0, :])
         nc.sync.dma_start(offsets[:], offs)
         nc.sync.dma_start(out=zp_cut[:], in_=zp[0:1, :].rearrange("o (p c) -> (o p) c", c=ZP_COLS))
-        for t in range(1, PACK):
-            nc.sync.dma_start(out=planes[t][:], in_=rows[:, t, :])
+        nc.sync.dma_start(out=middle[:], in_=rows[:, 1:3, :], max_dma_last_dim=4 * T)
+        nc.sync.dma_start(out=planes[3][:], in_=rows[:, 3, :])
+        windows = (planes[0][:], middle[:, 0, :], middle[:, 1, :], planes[3][:])
 
         w_codes = keep.tile([P, 2 * N], U8, name="w_codes", align_bytes=64)
         w_scales = keep.tile([P, N], U8, name="w_scales", align_bytes=64)
@@ -62,6 +63,9 @@ def tile_picked_zeropt_none_l_kernel(tc, xT, zp, csum, w1_words, w1_scales, offs
 
         nc.sync.dma_start(out=csum_col[:], in_=csum)
 
+        early = keep.tile([P, 2, S - OWN], F32, name="early")
+        nc.vector.tensor_copy(early[:, 0, :], windows[0].indirect(entries(0, S - OWN)))
+
         identity = keep.tile([P, P], F32, name="identity")
         make_identity(nc, identity[:])
 
@@ -75,28 +79,27 @@ def tile_picked_zeropt_none_l_kernel(tc, xT, zp, csum, w1_words, w1_scales, offs
             nc.scalar.copy(out=zp_runs[:, a, :, :], in_=bank[:].rearrange("p j n -> p n j"))
         zp_picked = keep.tile([P, S], F32, name="zp_picked")
         nc.scalar.activation(zp_picked[:], zp_table[:].indirect(offsets[:]), COPY)
+        nc.scalar.activation(early[:, 1, :], windows[1].indirect(entries(0, S - OWN)), COPY)
 
         picked_own = keep.tile([P, OWN, PACK], BF16, name="picked_own", align_bytes=64)
         runs = range((S - OWN) // RUN)
         picked = [keep.tile([P, RUN, PACK], BF16, name=f"picked{r}", align_bytes=64) for r in runs]
-        early = keep.tile([P, 2, S], BF16, name="early")
-        for t in range(2):
-            nc.vector.tensor_copy(early[:, t, :], planes[t][:].indirect(offsets[:]))
-        nc.vector.tensor_copy(out=picked_own[:, :, 0:2], in_=early[:, :, S - OWN - LAST : S - LAST].rearrange("p t c -> p c t"))
+        own_first = S - OWN
 
         def first_of(r):
-            return r * RUN if r * RUN < S - OWN - LAST else OWN + r * RUN
+            return r * RUN
 
-        own_first = S - OWN - LAST
-        shared = keep.tile([P, 3, RUN], BF16, name="late_shared", align_bytes=64)
-        late1 = keep.tile([P, 2, RUN], BF16, name="late1", tag="late1", align_bytes=64)
-        late2 = keep.tile([P, 2, RUN], BF16, name="late2", align_bytes=64)
+        for r in runs:
+            nc.gpsimd.tensor_scalar(picked[r][:, :, 0:2], early[:, :, first_of(r) : first_of(r) + RUN].rearrange("p t c -> p c t"), 1.0, 0.0, MULT, ADD)
+
+        shared = keep.tile([P, 3, RUN], F32, name="late_shared", align_bytes=64)
+        late1 = keep.tile([P, 2, RUN], F32, name="late1", tag="late1", align_bytes=64)
+        late2 = keep.tile([P, 2, RUN], F32, name="late2", align_bytes=64)
         late = (shared[:, 1:3, :], late1[:], late2[:], shared[:, 0:2, :])
         for r in runs:
-            nc.vector.tensor_copy(out=picked[r][:, :, 0:2], in_=early[:, :, first_of(r) : first_of(r) + RUN].rearrange("p t c -> p c t"))
-            nc.vector.tensor_copy(late[r][:, 0, :], planes[2][:].indirect(entries(first_of(r), RUN)))
-        for t in (2, 3):
-            nc.vector.tensor_copy(picked_own[:, :, t], planes[t][:].indirect(entries(own_first, OWN)))
+            nc.scalar.activation(late[r][:, 0, :], windows[2].indirect(entries(first_of(r), RUN)), COPY)
+        for t in range(PACK):
+            nc.vector.tensor_copy(picked_own[:, :, t], windows[t].indirect(entries(own_first, OWN)))
 
         def fetch(r):
             nc.scalar.activation(late[r][:, 1, :], planes[3][:].indirect(entries(first_of(r), RUN)), COPY)
@@ -117,7 +120,7 @@ def tile_picked_zeropt_none_l_kernel(tc, xT, zp, csum, w1_words, w1_scales, offs
         sums = {}
 
         def multiply(first, count, source, x_codes, y):
-            tag = "csum" if first == S - RUN else f"x_scales{first}"
+            tag = "csum" if first == first_of(3) else f"x_scales{first}"
             x_scales = keep.tile([P, count], U8, name=f"x_scales{first}", tag=tag, align_bytes=64)
             nc.vector.quantize_mx(
                 out=x_codes.bitcast(FP8X4),

@@ -89,15 +89,19 @@ def tile_picked_zeropt_none_l_kernel(tc, xT, zp, csum, w1_words, w1_scales, offs
         def first_of(r):
             return r * RUN
 
-        for r in runs:
-            nc.gpsimd.tensor_scalar(picked[r][:, :, 0:2], early[:, :, first_of(r) : first_of(r) + RUN].rearrange("p t c -> p c t"), 1.0, 0.0, MULT, ADD)
+        first_pairs = [early[:, :, first_of(r) : first_of(r) + RUN].rearrange("p t c -> p c t") for r in runs]
+        for r in range(3):
+            nc.gpsimd.tensor_scalar(picked[r][:, :, 0:2], first_pairs[r], 1.0, 0.0, MULT, ADD)
 
-        shared = keep.tile([P, 3, RUN], F32, name="late_shared", align_bytes=64)
-        late1 = keep.tile([P, 2, RUN], F32, name="late1", tag="late1", align_bytes=64)
-        late2 = keep.tile([P, 2, RUN], F32, name="late2", align_bytes=64)
+        shared = keep.tile([P, 3, RUN], BF16, name="late_shared", align_bytes=64)
+        late1 = keep.tile([P, 2, RUN], BF16, name="late1", tag="late1", align_bytes=64)
+        late2 = keep.tile([P, 2, RUN], BF16, name="late2", align_bytes=64)
         late = (shared[:, 1:3, :], late1[:], late2[:], shared[:, 0:2, :])
+        third = keep.tile([P, S - OWN], F32, name="third")
+        nc.scalar.activation(third[:], windows[2].indirect(entries(0, S - OWN)), COPY)
         for r in runs:
-            nc.scalar.activation(late[r][:, 0, :], windows[2].indirect(entries(first_of(r), RUN)), COPY)
+            nc.scalar.copy(out=late[r][:, 0, :], in_=third[:, first_of(r) : first_of(r) + RUN])
+        nc.scalar.copy(out=picked[3][:, :, 0:2], in_=first_pairs[3])
         for t in range(PACK):
             nc.vector.tensor_copy(picked_own[:, :, t], windows[t].indirect(entries(own_first, OWN)))
 

@@ -40,15 +40,14 @@ def tile_picked_zeropt_none_l_kernel(tc, xT, zp, csum, w1_words, w1_scales, offs
             return offsets[:, first // 16 : (first + count) // 16]
 
         rows = xT.rearrange("(p t) w -> p t w", t=PACK)
-        middle = keep.tile([P, 2, T], F32, name="middle")
-        planes = {t: keep.tile([P, T], F32, name=f"plane{t}") for t in (0, 3)}
+        planes = [keep.tile([P, T], F32, name=f"plane{t}") for t in range(PACK)]
         zp_cut = keep.tile([P, ZP_COLS], F32, name="zp_cut")
         nc.sync.dma_start(out=planes[0][:], in_=rows[:, 0, :])
         nc.sync.dma_start(offsets[:], offs)
         nc.sync.dma_start(out=zp_cut[:], in_=zp[0:1, :].rearrange("o (p c) -> (o p) c", c=ZP_COLS))
-        nc.sync.dma_start(out=middle[:], in_=rows[:, 1:3, :], max_dma_last_dim=4 * T)
-        nc.sync.dma_start(out=planes[3][:], in_=rows[:, 3, :])
-        windows = (planes[0][:], middle[:, 0, :], middle[:, 1, :], planes[3][:])
+        for t in range(1, PACK):
+            nc.sync.dma_start(out=planes[t][:], in_=rows[:, t, :])
+        windows = [plane[:] for plane in planes]
 
         w_codes = keep.tile([P, 2 * N], U8, name="w_codes", align_bytes=64)
         w_scales = keep.tile([P, N], U8, name="w_scales", align_bytes=64)

@@ -40,14 +40,15 @@ def tile_picked_zeropt_none_l_kernel(tc, xT, zp, csum, w1_words, w1_scales, offs
             return offsets[:, first // 16 : (first + count) // 16]
 
         rows = xT.rearrange("(p t) w -> p t w", t=PACK)
-        planes = [keep.tile([P, T], F32, name=f"plane{t}") for t in range(PACK)]
+        front = keep.tile([P, 2, T], F32, name="front")
+        planes = {t: keep.tile([P, T], F32, name=f"plane{t}") for t in (2, 3)}
         zp_cut = keep.tile([P, ZP_COLS], F32, name="zp_cut")
-        nc.sync.dma_start(out=planes[0][:], in_=rows[:, 0, :])
+        nc.sync.dma_start(out=planes[2][:], in_=rows[:, 2, :])
         nc.sync.dma_start(offsets[:], offs)
         nc.sync.dma_start(out=zp_cut[:], in_=zp[0:1, :].rearrange("o (p c) -> (o p) c", c=ZP_COLS))
-        for t in range(1, PACK):
-            nc.sync.dma_start(out=planes[t][:], in_=rows[:, t, :])
-        windows = [plane[:] for plane in planes]
+        nc.sync.dma_start(out=front[:], in_=rows[:, 0:2, :])
+        nc.sync.dma_start(out=planes[3][:], in_=rows[:, 3, :])
+        windows = (front[:, 0, :], front[:, 1, :], planes[2][:], planes[3][:])
 
         w_codes = keep.tile([P, 2 * N], U8, name="w_codes", align_bytes=64)
         w_scales = keep.tile([P, N], U8, name="w_scales", align_bytes=64)
@@ -63,7 +64,6 @@ def tile_picked_zeropt_none_l_kernel(tc, xT, zp, csum, w1_words, w1_scales, offs
         nc.sync.dma_start(out=csum_col[:], in_=csum)
 
         early = keep.tile([P, 2, S - OWN], F32, name="early")
-        nc.vector.tensor_copy(early[:, 0, :], windows[0].indirect(entries(0, S - OWN)))
 
         identity = keep.tile([P, P], F32, name="identity")
         make_identity(nc, identity[:])
@@ -78,7 +78,8 @@ def tile_picked_zeropt_none_l_kernel(tc, xT, zp, csum, w1_words, w1_scales, offs
             nc.scalar.copy(out=zp_runs[:, a, :, :], in_=bank[:].rearrange("p j n -> p n j"))
         zp_picked = keep.tile([P, S], F32, name="zp_picked")
         nc.scalar.activation(zp_picked[:], zp_table[:].indirect(offsets[:]), COPY)
-        nc.scalar.activation(early[:, 1, :], windows[1].indirect(entries(0, S - OWN)), COPY)
+        for t in range(2):
+            nc.scalar.activation(early[:, t, :], windows[t].indirect(entries(0, S - OWN)), COPY)
 
         picked_own = keep.tile([P, OWN, PACK], BF16, name="picked_own", align_bytes=64)
         runs = range((S - OWN) // RUN)
@@ -89,20 +90,20 @@ def tile_picked_zeropt_none_l_kernel(tc, xT, zp, csum, w1_words, w1_scales, offs
             return r * RUN
 
         first_pairs = [early[:, :, first_of(r) : first_of(r) + RUN].rearrange("p t c -> p c t") for r in runs]
-        for r in range(3):
-            nc.gpsimd.tensor_scalar(picked[r][:, :, 0:2], first_pairs[r], 1.0, 0.0, MULT, ADD)
 
         shared = keep.tile([P, 3, RUN], BF16, name="late_shared", align_bytes=64)
         late1 = keep.tile([P, 2, RUN], BF16, name="late1", tag="late1", align_bytes=64)
         late2 = keep.tile([P, 2, RUN], BF16, name="late2", align_bytes=64)
         late = (shared[:, 1:3, :], late1[:], late2[:], shared[:, 0:2, :])
-        third = keep.tile([P, S - OWN], F32, name="third")
-        nc.scalar.activation(third[:], windows[2].indirect(entries(0, S - OWN)), COPY)
         for r in runs:
-            nc.scalar.copy(out=late[r][:, 0, :], in_=third[:, first_of(r) : first_of(r) + RUN])
-        nc.scalar.copy(out=picked[3][:, :, 0:2], in_=first_pairs[3])
-        for t in range(PACK):
+            nc.vector.tensor_copy(late[r][:, 0, :], windows[2].indirect(entries(first_of(r), RUN)))
+        for t in (2, 0, 1):
             nc.vector.tensor_copy(picked_own[:, :, t], windows[t].indirect(entries(own_first, OWN)))
+        for r in (0, 3):
+            nc.scalar.copy(out=picked[r][:, :, 0:2], in_=first_pairs[r])
+        for r in (1, 2):
+            nc.vector.tensor_copy(out=picked[r][:, :, 0:2], in_=first_pairs[r])
+        nc.vector.tensor_copy(picked_own[:, :, 3], windows[3].indirect(entries(own_first, OWN)))
 
         def fetch(r):
             nc.scalar.activation(late[r][:, 1, :], planes[3][:].indirect(entries(first_of(r), RUN)), COPY)

@@ -42,10 +42,10 @@ def tile_picked_zeropt_none_l_kernel(tc, xT, zp, csum, w1_words, w1_scales, offs
         rows = xT.rearrange("(p t) w -> p t w", t=PACK)
         front = keep.tile([P, 2, T], F32, name="front")
         planes = {t: keep.tile([P, T], F32, name=f"plane{t}") for t in (2, 3)}
-        zp_cut = keep.tile([P, ZP_COLS], F32, name="zp_cut")
+        zp_rows = keep.tile([P, P], F32, name="zp_rows")
         nc.sync.dma_start(out=planes[2][:], in_=rows[:, 2, :])
         nc.sync.dma_start(offsets[:], offs)
-        nc.sync.dma_start(out=zp_cut[:], in_=zp[0:1, :].rearrange("o (p c) -> (o p) c", c=ZP_COLS))
+        nc.sync.dma_start(out=zp_rows[:ZP_COLS, :], in_=zp[0:1, :].rearrange("o (r c) -> (o r) c", c=P))
         nc.sync.dma_start(out=front[:], in_=rows[:, 0:2, :])
         nc.sync.dma_start(out=planes[3][:], in_=rows[:, 3, :])
         windows = (front[:, 0, :], front[:, 1, :], planes[2][:], planes[3][:])
@@ -54,7 +54,8 @@ def tile_picked_zeropt_none_l_kernel(tc, xT, zp, csum, w1_words, w1_scales, offs
         w_scales = keep.tile([P, N], U8, name="w_scales", align_bytes=64)
         csum_col = keep.tile([P, 1], F32, name="csum_col", tag="csum", align_bytes=64)
         nc.gpsimd.memset(w_scales[:].bitcast(I32), 0)
-        nc.sync.dma_start(out=w_codes[:].bitcast(I32), in_=w1_words[0].bitcast(I32))
+        for first in (0, N):
+            nc.sync.dma_start(out=w_codes[:, first : first + N].bitcast(I32), in_=w1_words[0, :, first : first + N].bitcast(I32))
         for q in range(4):
             nc.sync.dma_start(
                 out=w_scales[32 * q : 32 * q + 4, :].bitcast(I32),
@@ -68,14 +69,20 @@ def tile_picked_zeropt_none_l_kernel(tc, xT, zp, csum, w1_words, w1_scales, offs
         identity = keep.tile([P, P], F32, name="identity")
         make_identity(nc, identity[:])
 
+        nc.vector.memset(zp_rows[ZP_COLS : 2 * ZP_COLS, :], 0.0)
+        nc.vector.memset(zp_rows[2 * ZP_COLS :, :], 0.0)
+        turned = zbanks.tile([P, BANK_SLOTS, P], F32, name="zbank")
+        nc.tensor.transpose(turned[:, 0, :], zp_rows[:], identity[:])
+        zp_cut = keep.tile([P, ZP_COLS], F32, name="zp_cut")
+        nc.scalar.copy(out=zp_cut[:], in_=turned[:, 0, :ZP_COLS])
+
         zp_table = keep.tile([P, T], F32, name="zp_table")
-        zp_runs = zp_table[:].rearrange("p (n a j) -> p a n j", a=ZP_COLS // BANK_SLOTS, j=BANK_SLOTS)
         for a in range(ZP_COLS // BANK_SLOTS):
             bank = zbanks.tile([P, BANK_SLOTS, P], F32, name="zbank")
             for j in range(BANK_SLOTS):
                 c = BANK_SLOTS * a + j
                 nc.tensor.transpose(bank[:, j, :], zp_cut[:, c : c + 1].to_broadcast([P, P]), identity[:])
-            nc.scalar.copy(out=zp_runs[:, a, :, :], in_=bank[:].rearrange("p j n -> p n j"))
+            nc.scalar.copy(out=zp_table[:, a * BANK_SLOTS * P : (a + 1) * BANK_SLOTS * P], in_=bank[:].rearrange("p j n -> p (j n)"))
         zp_picked = keep.tile([P, S], F32, name="zp_picked")
         nc.scalar.activation(zp_picked[:], zp_table[:].indirect(offsets[:]), COPY)
         for t in range(2):

@@ -24,14 +24,14 @@ ZP_COLS = T // P
 BANK_SLOTS = 4
 STORE = 256
 RUN = 128
-OWN = 512
+OWN = 256
 
 
 def tile_picked_zeropt_none_l_kernel(tc, xT, zp, csum, w1_words, w1_scales, offs, out):
     nc = tc.nc
     with ExitStack() as ctx:
         keep = ctx.enter_context(tc.tile_pool(name="keep", bufs=1))
-        zbanks = ctx.enter_context(tc.psum_pool(name="zbanks", bufs=4))
+        zbanks = ctx.enter_context(tc.psum_pool(name="zbanks", bufs=3))
         ybanks = ctx.enter_context(tc.psum_pool(name="ybanks", bufs=1))
 
         offsets = keep.tile([P, S // 16], U16, name="offsets")
@@ -40,31 +40,25 @@ def tile_picked_zeropt_none_l_kernel(tc, xT, zp, csum, w1_words, w1_scales, offs
             return offsets[:, first // 16 : (first + count) // 16]
 
         rows = xT.rearrange("(p t) w -> p t w", t=PACK)
-        front = keep.tile([P, 2, T], F32, name="front")
-        planes = {t: keep.tile([P, T], F32, name=f"plane{t}") for t in (2, 3)}
+        planes = [keep.tile([P, T], F32, name=f"plane{t}") for t in range(PACK)]
         zp_rows = keep.tile([P, P], F32, name="zp_rows")
-        nc.sync.dma_start(out=planes[2][:], in_=rows[:, 2, :])
+        nc.sync.dma_start(out=planes[0][:], in_=rows[:, 0, :])
         nc.sync.dma_start(offsets[:], offs)
         nc.sync.dma_start(out=zp_rows[:ZP_COLS, :], in_=zp[0:1, :].rearrange("o (r c) -> (o r) c", c=P))
-        nc.sync.dma_start(out=front[:], in_=rows[:, 0:2, :])
-        nc.sync.dma_start(out=planes[3][:], in_=rows[:, 3, :])
-        windows = (front[:, 0, :], front[:, 1, :], planes[2][:], planes[3][:])
+        for t in range(1, PACK):
+            nc.sync.dma_start(out=planes[t][:], in_=rows[:, t, :])
 
         w_codes = keep.tile([P, 2 * N], U8, name="w_codes", align_bytes=64)
         w_scales = keep.tile([P, N], U8, name="w_scales", align_bytes=64)
-        csum_col = keep.tile([P, 1], F32, name="csum_col", tag="csum", align_bytes=64)
+        csum_col = keep.tile([P, 1], F32, name="csum_col")
         nc.gpsimd.memset(w_scales[:].bitcast(I32), 0)
-        for first in (0, N):
-            nc.sync.dma_start(out=w_codes[:, first : first + N].bitcast(I32), in_=w1_words[0, :, first : first + N].bitcast(I32))
+        nc.sync.dma_start(out=csum_col[:], in_=csum)
+        nc.sync.dma_start(out=w_codes[:].bitcast(I32), in_=w1_words[0].bitcast(I32))
         for q in range(4):
             nc.sync.dma_start(
                 out=w_scales[32 * q : 32 * q + 4, :].bitcast(I32),
                 in_=w1_scales[0, 4 * q : 4 * q + 4, :].bitcast(I32),
             )
-
-        nc.sync.dma_start(out=csum_col[:], in_=csum)
-
-        early = keep.tile([P, 2, S - OWN], F32, name="early")
 
         identity = keep.tile([P, P], F32, name="identity")
         make_identity(nc, identity[:])
@@ -83,92 +77,87 @@ def tile_picked_zeropt_none_l_kernel(tc, xT, zp, csum, w1_words, w1_scales, offs
                 c = BANK_SLOTS * a + j
                 nc.tensor.transpose(bank[:, j, :], zp_cut[:, c : c + 1].to_broadcast([P, P]), identity[:])
             nc.scalar.copy(out=zp_table[:, a * BANK_SLOTS * P : (a + 1) * BANK_SLOTS * P], in_=bank[:].rearrange("p j n -> p (j n)"))
-        zp_picked = keep.tile([P, S], F32, name="zp_picked")
-        nc.scalar.activation(zp_picked[:], zp_table[:].indirect(offsets[:]), COPY)
-        for t in range(2):
-            nc.scalar.activation(early[:, t, :], windows[t].indirect(entries(0, S - OWN)), COPY)
+        zp_negated = keep.tile([P, S], F32, name="zp_negated")
+        nc.scalar.activation(zp_negated[:], zp_table[:].indirect(offsets[:]), COPY, scale=-1.0)
 
-        picked_own = keep.tile([P, OWN, PACK], BF16, name="picked_own", align_bytes=64)
-        runs = range((S - OWN) // RUN)
-        picked = [keep.tile([P, RUN, PACK], BF16, name=f"picked{r}", align_bytes=64) for r in runs]
+        picked = keep.tile([P, S, PACK], BF16, name="picked", align_bytes=64)
         own_first = S - OWN
+        runs = range(own_first // RUN)
+        staged = keep.tile([P, 2, OWN], BF16, name="staged", align_bytes=64)
 
-        def first_of(r):
-            return r * RUN
+        for t in range(2):
+            nc.vector.tensor_copy(picked[:, :, t], planes[t][:].indirect(offsets[:]))
+        nc.scalar.activation(picked[:, :own_first, 2], planes[2][:].indirect(entries(0, own_first)), COPY)
+        nc.vector.tensor_copy(staged[:, 0, :], planes[2][:].indirect(entries(own_first, OWN)))
+        for at in range(0, OWN, RUN):
+            nc.vector.tensor_copy(staged[:, 1, at : at + RUN], planes[3][:].indirect(entries(own_first + at, RUN)))
 
-        first_pairs = [early[:, :, first_of(r) : first_of(r) + RUN].rearrange("p t c -> p c t") for r in runs]
+        def lay(at):
+            nc.vector.tensor_copy(out=picked[:, own_first + at : own_first + at + RUN, 2:4], in_=staged[:, :, at : at + RUN].rearrange("p t c -> p c t"))
 
-        shared = keep.tile([P, 3, RUN], BF16, name="late_shared", align_bytes=64)
-        late1 = keep.tile([P, 2, RUN], BF16, name="late1", tag="late1", align_bytes=64)
-        late2 = keep.tile([P, 2, RUN], BF16, name="late2", align_bytes=64)
-        late = (shared[:, 1:3, :], late1[:], late2[:], shared[:, 0:2, :])
         for r in runs:
-            nc.vector.tensor_copy(late[r][:, 0, :], windows[2].indirect(entries(first_of(r), RUN)))
-        for t in (2, 0, 1):
-            nc.vector.tensor_copy(picked_own[:, :, t], windows[t].indirect(entries(own_first, OWN)))
-        for r in (0, 3):
-            nc.scalar.copy(out=picked[r][:, :, 0:2], in_=first_pairs[r])
-        for r in (1, 2):
-            nc.vector.tensor_copy(out=picked[r][:, :, 0:2], in_=first_pairs[r])
-        nc.vector.tensor_copy(picked_own[:, :, 3], windows[3].indirect(entries(own_first, OWN)))
+            nc.scalar.activation(picked[:, r * RUN : (r + 1) * RUN, 3], planes[3][:].indirect(entries(r * RUN, RUN)), COPY)
 
-        def fetch(r):
-            nc.scalar.activation(late[r][:, 1, :], planes[3][:].indirect(entries(first_of(r), RUN)), COPY)
-
-        def lay(r):
-            nc.scalar.copy(out=picked[r][:, :, 2:4], in_=late[r].rearrange("p t c -> p c t"))
-
-        for r in range(3):
-            fetch(r)
-        nc.gpsimd.tensor_scalar(picked[0][:, :, 2:4], late[0].rearrange("p t c -> p c t"), 1.0, 0.0, MULT, ADD)
-        csum_negated = keep.tile([P, 1], F32, name="csum_negated")
-        nc.gpsimd.tensor_scalar(csum_negated[:], csum_col[:], -1.0, 0.0, MULT, ADD)
-        lay(1)
-        fetch(3)
-        for r in (2, 3):
-            lay(r)
-
-        sums = {}
-
-        def multiply(first, count, source, x_codes, y):
-            tag = "csum" if first == first_of(3) else f"x_scales{first}"
-            x_scales = keep.tile([P, count], U8, name=f"x_scales{first}", tag=tag, align_bytes=64)
+        def quantise(first, count, x_codes, x_scales):
             nc.vector.quantize_mx(
                 out=x_codes.bitcast(FP8X4),
-                scales=x_scales[:],
-                in_=source.rearrange("p c t -> p (c t)"),
+                scales=x_scales,
+                in_=picked[:, first : first + count, :].rearrange("p c t -> p (c t)"),
             )
-            sums[first] = y
+
+        def multiply(x_codes, x_scales, y):
             nc.tensor.matmul_mx(
                 out=y,
                 lhsT=w_codes[:].bitcast(FP4X4),
                 lhsT_scale=w_scales[:],
                 rhs=x_codes.bitcast(FP8X4),
-                rhs_scale=x_scales[:],
+                rhs_scale=x_scales,
                 start=True,
                 stop=True,
             )
 
         results = [keep.tile([P, STORE], F32, name=f"result{j}") for j in range(S // STORE)]
 
-        def correct(first, count):
+        def correct(first, count, y):
             j, at = divmod(first, STORE)
-            nc.vector.scalar_tensor_tensor(results[j][:, at : at + count], zp_picked[:, first : first + count], csum_negated[:, 0:1], sums[first], MULT, ADD)
+            nc.vector.scalar_tensor_tensor(results[j][:, at : at + count], zp_negated[:, first : first + count], csum_col[:, 0:1], y, MULT, ADD)
             if at + count == STORE:
                 nc.sync.dma_start(out=out[:, j * STORE : (j + 1) * STORE], in_=results[j][:])
 
-        run_codes = [keep.tile([P, RUN], U32, name=f"run_codes{r}", align_bytes=64) for r in range(3)]
-        y_first = ybanks.tile([P, STORE], F32, name="y_first")
-        for r in (0, 1):
-            multiply(first_of(r), RUN, picked[r][:], run_codes[r][:], y_first[:, r * RUN : (r + 1) * RUN])
-        sums[0] = y_first[:]
-        own_codes = keep.tile([P, OWN], U32, name="own_codes", tag="late1", align_bytes=64)
-        for h in range(2):
-            multiply(own_first + h * STORE, STORE, picked_own[:, h * STORE : (h + 1) * STORE, :], own_codes[:, h * STORE : (h + 1) * STORE], ybanks.tile([P, STORE], F32, name=f"y_own{h}")[:])
-        multiply(first_of(2), RUN, picked[2][:], run_codes[2][:], zbanks.tile([P, BANK_SLOTS, P], F32, name="zbank")[:, 0, :])
-        correct(0, STORE)
-        multiply(first_of(3), RUN, picked[3][:], run_codes[1][:], zbanks.tile([P, BANK_SLOTS, P], F32, name="zbank")[:, 0, :])
-        for h in range(2):
-            correct(own_first + h * STORE, STORE)
-        for r in (2, 3):
-            correct(first_of(r), RUN)
+        pair_sums = [ybanks.tile([P, STORE], F32, name=f"y_pair{h}") for h in range(2)]
+        own_sums = ybanks.tile([P, OWN], F32, name="y_own")
+        last_sums = [ybanks.tile([P, RUN], F32, name=f"y_last{h}") for h in range(2)]
+
+        def run_sums(r):
+            if r < 4:
+                return pair_sums[r // 2][:, (r % 2) * RUN : (r % 2 + 1) * RUN]
+            return last_sums[r - 4][:]
+
+        def operand(name, count):
+            codes = keep.tile([P, count], U32, name=f"{name}_codes", align_bytes=64)
+            scales = keep.tile([P, count], U8, name=f"{name}_scales", align_bytes=64)
+            return codes, scales
+
+        def run_product(r, codes, scales):
+            quantise(r * RUN, RUN, codes, scales)
+            multiply(codes, scales, run_sums(r))
+
+        first_codes, first_scales = operand("first", 2 * RUN)
+        own_codes, own_scales = operand("own", OWN)
+        third_codes, third_scales = operand("third", RUN)
+        lay(0)
+        quantise(0, RUN, first_codes[:, :RUN], first_scales[:, :RUN])
+        lay(RUN)
+        quantise(RUN, RUN, first_codes[:, RUN:], first_scales[:, RUN:])
+        multiply(first_codes[:], first_scales[:], pair_sums[0][:])
+        quantise(own_first, OWN, own_codes[:], own_scales[:])
+        multiply(own_codes[:], own_scales[:], own_sums[:])
+        run_product(2, third_codes[:], third_scales[:])
+        correct(0, STORE, pair_sums[0][:])
+        run_product(3, first_codes[:, :RUN], first_scales[:, :RUN])
+        run_product(4, first_codes[:, RUN:], first_scales[:, RUN:])
+        correct(own_first, OWN, own_sums[:])
+        run_product(5, own_codes[:, :RUN], own_scales[:, :RUN])
+        correct(STORE, STORE, pair_sums[1][:])
+        for r in (4, 5):
+            correct(r * RUN, RUN, run_sums(r))

@@ -116,7 +116,7 @@ def tile_picked_zeropt_none_l_kernel(tc, xT, zp, csum, w1_words, w1_scales, offs
                 stop=True,
             )
 
-        results = [keep.tile([P, STORE], F32, name=f"result{j}") for j in range(S // STORE)]
+        results = [keep.tile([P, STORE], F32, name=f"result{j}", align_bytes=256) for j in range(S // STORE)]
 
         def correct(first, count, y):
             j, at = divmod(first, STORE)

@@ -24,7 +24,8 @@ ZP_COLS = T // P
 BANK_SLOTS = 4
 STORE = 256
 RUN = 128
-OWN = 256
+OWN_FIRST = 256
+OWN = 320
 
 
 def tile_picked_zeropt_none_l_kernel(tc, xT, zp, csum, w1_words, w1_scales, offs, out):
@@ -81,33 +82,37 @@ def tile_picked_zeropt_none_l_kernel(tc, xT, zp, csum, w1_words, w1_scales, offs
         nc.scalar.activation(zp_negated[:], zp_table[:].indirect(offsets[:]), COPY, scale=-1.0)
 
         picked = keep.tile([P, S, PACK], BF16, name="picked", align_bytes=64)
-        own_first = S - OWN
-        runs = range(own_first // RUN)
         staged = keep.tile([P, 2, OWN], BF16, name="staged", align_bytes=64)
+        own_end = OWN_FIRST + OWN
+        own_half = OWN // 2
+
+        def place(t, first, end):
+            nc.scalar.activation(picked[:, first:end, t], planes[t][:].indirect(entries(first, end - first)), COPY)
 
         for t in range(2):
             nc.vector.tensor_copy(picked[:, :, t], planes[t][:].indirect(offsets[:]))
-        nc.scalar.activation(picked[:, :own_first, 2], planes[2][:].indirect(entries(0, own_first)), COPY)
-        nc.vector.tensor_copy(staged[:, 0, :], planes[2][:].indirect(entries(own_first, OWN)))
-        for at in range(0, OWN, RUN):
-            nc.vector.tensor_copy(staged[:, 1, at : at + RUN], planes[3][:].indirect(entries(own_first + at, RUN)))
+        place(2, 0, OWN_FIRST)
+        place(2, own_end, S)
+        nc.vector.tensor_copy(staged[:, 0, :], planes[2][:].indirect(entries(OWN_FIRST, OWN)))
+        for at in (0, own_half):
+            nc.vector.tensor_copy(staged[:, 1, at : at + own_half], planes[3][:].indirect(entries(OWN_FIRST + at, own_half)))
+        for first, end in ((0, OWN_FIRST), (own_end, 3 * STORE), (3 * STORE, S - RUN), (S - RUN, S)):
+            place(3, first, end)
+        for at in (0, own_half):
+            nc.vector.tensor_copy(
+                out=picked[:, OWN_FIRST + at : OWN_FIRST + at + own_half, 2:4],
+                in_=staged[:, :, at : at + own_half].rearrange("p t c -> p c t"),
+            )
 
-        def lay(at):
-            nc.vector.tensor_copy(out=picked[:, own_first + at : own_first + at + RUN, 2:4], in_=staged[:, :, at : at + RUN].rearrange("p t c -> p c t"))
-
-        for r in runs:
-            nc.scalar.activation(picked[:, r * RUN : (r + 1) * RUN, 3], planes[3][:].indirect(entries(r * RUN, RUN)), COPY)
-
-        def quantise(first, count, x_codes, x_scales):
+        def product(first, count, x_codes, x_scales):
             nc.vector.quantize_mx(
                 out=x_codes.bitcast(FP8X4),
                 scales=x_scales,
                 in_=picked[:, first : first + count, :].rearrange("p c t -> p (c t)"),
             )
-
-        def multiply(x_codes, x_scales, y):
+            y = ybanks.tile([P, count], F32, name=f"y{first}")
             nc.tensor.matmul_mx(
-                out=y,
+                out=y[:],
                 lhsT=w_codes[:].bitcast(FP4X4),
                 lhsT_scale=w_scales[:],
                 rhs=x_codes.bitcast(FP8X4),
@@ -115,49 +120,23 @@ def tile_picked_zeropt_none_l_kernel(tc, xT, zp, csum, w1_words, w1_scales, offs
                 start=True,
                 stop=True,
             )
+            return y
 
         results = [keep.tile([P, STORE], F32, name=f"result{j}", align_bytes=256) for j in range(S // STORE)]
 
         def correct(first, count, y):
             j, at = divmod(first, STORE)
-            nc.vector.scalar_tensor_tensor(results[j][:, at : at + count], zp_negated[:, first : first + count], csum_col[:, 0:1], y, MULT, ADD)
+            nc.vector.scalar_tensor_tensor(results[j][:, at : at + count], zp_negated[:, first : first + count], csum_col[:, 0:1], y[:], MULT, ADD)
             if at + count == STORE:
                 nc.sync.dma_start(out=out[:, j * STORE : (j + 1) * STORE], in_=results[j][:])
 
-        pair_sums = [ybanks.tile([P, STORE], F32, name=f"y_pair{h}") for h in range(2)]
-        own_sums = ybanks.tile([P, OWN], F32, name="y_own")
-        last_sums = [ybanks.tile([P, RUN], F32, name=f"y_last{h}") for h in range(2)]
-
-        def run_sums(r):
-            if r < 4:
-                return pair_sums[r // 2][:, (r % 2) * RUN : (r % 2 + 1) * RUN]
-            return last_sums[r - 4][:]
-
-        def operand(name, count):
-            codes = keep.tile([P, count], U32, name=f"{name}_codes", align_bytes=64)
-            scales = keep.tile([P, count], U8, name=f"{name}_scales", align_bytes=64)
-            return codes, scales
-
-        def run_product(r, codes, scales):
-            quantise(r * RUN, RUN, codes, scales)
-            multiply(codes, scales, run_sums(r))
-
-        first_codes, first_scales = operand("first", 2 * RUN)
-        own_codes, own_scales = operand("own", OWN)
-        third_codes, third_scales = operand("third", RUN)
-        lay(0)
-        quantise(0, RUN, first_codes[:, :RUN], first_scales[:, :RUN])
-        lay(RUN)
-        quantise(RUN, RUN, first_codes[:, RUN:], first_scales[:, RUN:])
-        multiply(first_codes[:], first_scales[:], pair_sums[0][:])
-        quantise(own_first, OWN, own_codes[:], own_scales[:])
-        multiply(own_codes[:], own_scales[:], own_sums[:])
-        run_product(2, third_codes[:], third_scales[:])
-        correct(0, STORE, pair_sums[0][:])
-        run_product(3, first_codes[:, :RUN], first_scales[:, :RUN])
-        run_product(4, first_codes[:, RUN:], first_scales[:, RUN:])
-        correct(own_first, OWN, own_sums[:])
-        run_product(5, own_codes[:, :RUN], own_scales[:, :RUN])
-        correct(STORE, STORE, pair_sums[1][:])
-        for r in (4, 5):
-            correct(r * RUN, RUN, run_sums(r))
+        codes = [keep.tile([P, STORE], U32, name=f"codes{j}", align_bytes=64) for j in range(3)]
+        scales = [keep.tile([P, STORE], U8, name=f"scales{j}", align_bytes=64) for j in range(3)]
+        wide = [product(j * STORE, STORE, codes[j][:], scales[j][:]) for j in range(3)]
+        narrow = []
+        for j in range(2):
+            correct(j * STORE, STORE, wide[j])
+            narrow.append(product(3 * STORE + j * RUN, RUN, codes[j][:, :RUN], scales[j][:, :RUN]))
+        correct(2 * STORE, STORE, wide[2])
+        for j in range(2):
+            correct(3 * STORE + j * RUN, RUN, narrow[j])

@@ -94,15 +94,13 @@ def tile_picked_zeropt_none_l_kernel(tc, xT, zp, csum, w1_words, w1_scales, offs
         place(2, 0, OWN_FIRST)
         place(2, own_end, S)
         nc.vector.tensor_copy(staged[:, 0, :], planes[2][:].indirect(entries(OWN_FIRST, OWN)))
+        nc.vector.tensor_copy(out=picked[:, OWN_FIRST:own_end, 2], in_=staged[:, 0, :])
         for at in (0, own_half):
             nc.vector.tensor_copy(staged[:, 1, at : at + own_half], planes[3][:].indirect(entries(OWN_FIRST + at, own_half)))
         for first, end in ((0, OWN_FIRST), (own_end, 3 * STORE), (3 * STORE, S - RUN), (S - RUN, S)):
             place(3, first, end)
         for at in (0, own_half):
-            nc.vector.tensor_copy(
-                out=picked[:, OWN_FIRST + at : OWN_FIRST + at + own_half, 2:4],
-                in_=staged[:, :, at : at + own_half].rearrange("p t c -> p c t"),
-            )
+            nc.vector.tensor_copy(out=picked[:, OWN_FIRST + at : OWN_FIRST + at + own_half, 3], in_=staged[:, 1, at : at + own_half])
 
         def product(first, count, x_codes, x_scales):
             nc.vector.quantize_mx(

@@ -25,7 +25,7 @@ BANK_SLOTS = 4
 STORE = 256
 RUN = 128
 OWN_FIRST = 256
-OWN = 320
+OWN = 256
 
 
 def tile_picked_zeropt_none_l_kernel(tc, xT, zp, csum, w1_words, w1_scales, offs, out):
@@ -130,11 +130,13 @@ def tile_picked_zeropt_none_l_kernel(tc, xT, zp, csum, w1_words, w1_scales, offs
 
         codes = [keep.tile([P, STORE], U32, name=f"codes{j}", align_bytes=64) for j in range(3)]
         scales = [keep.tile([P, STORE], U8, name=f"scales{j}", align_bytes=64) for j in range(3)]
+        last_codes = keep.tile([P, RUN], U32, name="last_codes", align_bytes=64)
+        last_scales = keep.tile([P, RUN], U8, name="last_scales", align_bytes=64)
         wide = [product(j * STORE, STORE, codes[j][:], scales[j][:]) for j in range(3)]
-        narrow = []
-        for j in range(2):
+        narrow = [product(3 * STORE, RUN, last_codes[:], last_scales[:])]
+        correct(0, STORE, wide[0])
+        narrow.append(product(S - RUN, RUN, codes[0][:, :RUN], scales[0][:, :RUN]))
+        for j in (1, 2):
             correct(j * STORE, STORE, wide[j])
-            narrow.append(product(3 * STORE + j * RUN, RUN, codes[j][:, :RUN], scales[j][:, :RUN]))
-        correct(2 * STORE, STORE, wide[2])
         for j in range(2):
             correct(3 * STORE + j * RUN, RUN, narrow[j])

@@ -25,7 +25,7 @@ BANK_SLOTS = 4
 STORE = 256
 RUN = 128
 OWN_FIRST = 256
-OWN = 256
+OWN = 288
 
 
 def tile_picked_zeropt_none_l_kernel(tc, xT, zp, csum, w1_words, w1_scales, offs, out):
@@ -84,7 +84,7 @@ def tile_picked_zeropt_none_l_kernel(tc, xT, zp, csum, w1_words, w1_scales, offs
         picked = keep.tile([P, S, PACK], BF16, name="picked", align_bytes=64)
         staged = keep.tile([P, 2, OWN], BF16, name="staged", align_bytes=64)
         own_end = OWN_FIRST + OWN
-        own_half = OWN // 2
+        own_runs = ((0, OWN - RUN), (OWN - RUN, OWN))
 
         def place(t, first, end):
             nc.scalar.activation(picked[:, first:end, t], planes[t][:].indirect(entries(first, end - first)), COPY)
@@ -95,12 +95,12 @@ def tile_picked_zeropt_none_l_kernel(tc, xT, zp, csum, w1_words, w1_scales, offs
         place(2, own_end, S)
         nc.vector.tensor_copy(staged[:, 0, :], planes[2][:].indirect(entries(OWN_FIRST, OWN)))
         nc.vector.tensor_copy(out=picked[:, OWN_FIRST:own_end, 2], in_=staged[:, 0, :])
-        for at in (0, own_half):
-            nc.vector.tensor_copy(staged[:, 1, at : at + own_half], planes[3][:].indirect(entries(OWN_FIRST + at, own_half)))
+        for at, end in own_runs:
+            nc.vector.tensor_copy(staged[:, 1, at:end], planes[3][:].indirect(entries(OWN_FIRST + at, end - at)))
         for first, end in ((0, OWN_FIRST), (own_end, 3 * STORE), (3 * STORE, S - RUN), (S - RUN, S)):
             place(3, first, end)
-        for at in (0, own_half):
-            nc.vector.tensor_copy(out=picked[:, OWN_FIRST + at : OWN_FIRST + at + own_half, 3], in_=staged[:, 1, at : at + own_half])
+        for at, end in own_runs:
+            nc.vector.tensor_copy(out=picked[:, OWN_FIRST + at : OWN_FIRST + end, 3], in_=staged[:, 1, at:end])
 
         def product(first, count, x_codes, x_scales):
             nc.vector.quantize_mx(

from contextlib import ExitStack

import concourse.mybir as mybir
from concourse.masks import make_identity

K, T, S, N = 512, 4096, 1024, 128
FLOPS = 2 * K * N * S

F32 = mybir.dt.float32
BF16 = mybir.dt.bfloat16
I32 = mybir.dt.int32
U32 = mybir.dt.uint32
U16 = mybir.dt.uint16
U8 = mybir.dt.uint8
FP8X4 = mybir.dt.float8_e4m3fn_x4
FP4X4 = mybir.dt.float4_e2m1fn_x4
COPY = mybir.ActivationFunctionType.Copy
MULT = mybir.AluOpType.mult
ADD = mybir.AluOpType.add

P = 128
PACK = 4
ZP_COLS = T // P
BANK_SLOTS = 4
STORE = 256
RUN = 128
OWN_FIRST = 256
OWN = 288


def tile_picked_zeropt_none_l_kernel(tc, xT, zp, csum, w1_words, w1_scales, offs, out):
    nc = tc.nc
    with ExitStack() as ctx:
        keep = ctx.enter_context(tc.tile_pool(name="keep", bufs=1))
        zbanks = ctx.enter_context(tc.psum_pool(name="zbanks", bufs=3))
        ybanks = ctx.enter_context(tc.psum_pool(name="ybanks", bufs=1))

        offsets = keep.tile([P, S // 16], U16, name="offsets")

        def entries(first, count):
            return offsets[:, first // 16 : (first + count) // 16]

        rows = xT.rearrange("(p t) w -> p t w", t=PACK)
        planes = [keep.tile([P, T], F32, name=f"plane{t}") for t in range(PACK)]
        zp_rows = keep.tile([P, P], F32, name="zp_rows")
        nc.sync.dma_start(out=planes[0][:], in_=rows[:, 0, :])
        nc.sync.dma_start(offsets[:], offs)
        nc.sync.dma_start(out=zp_rows[:ZP_COLS, :], in_=zp[0:1, :].rearrange("o (r c) -> (o r) c", c=P))
        for t in range(1, PACK):
            nc.sync.dma_start(out=planes[t][:], in_=rows[:, t, :])

        w_codes = keep.tile([P, 2 * N], U8, name="w_codes", align_bytes=64)
        w_scales = keep.tile([P, N], U8, name="w_scales", align_bytes=64)
        csum_col = keep.tile([P, 1], F32, name="csum_col")
        nc.gpsimd.memset(w_scales[:].bitcast(I32), 0)
        nc.sync.dma_start(out=csum_col[:], in_=csum)
        nc.sync.dma_start(out=w_codes[:].bitcast(I32), in_=w1_words[0].bitcast(I32))
        for q in range(4):
            nc.sync.dma_start(
                out=w_scales[32 * q : 32 * q + 4, :].bitcast(I32),
                in_=w1_scales[0, 4 * q : 4 * q + 4, :].bitcast(I32),
            )

        identity = keep.tile([P, P], F32, name="identity")
        make_identity(nc, identity[:])

        nc.vector.memset(zp_rows[ZP_COLS : 2 * ZP_COLS, :], 0.0)
        nc.vector.memset(zp_rows[2 * ZP_COLS :, :], 0.0)
        turned = zbanks.tile([P, BANK_SLOTS, P], F32, name="zbank")
        nc.tensor.transpose(turned[:, 0, :], zp_rows[:], identity[:])
        zp_cut = keep.tile([P, ZP_COLS], F32, name="zp_cut")
        nc.scalar.copy(out=zp_cut[:], in_=turned[:, 0, :ZP_COLS])

        zp_table = keep.tile([P, T], F32, name="zp_table")
        for a in range(ZP_COLS // BANK_SLOTS):
            bank = zbanks.tile([P, BANK_SLOTS, P], F32, name="zbank")
            for j in range(BANK_SLOTS):
                c = BANK_SLOTS * a + j
                nc.tensor.transpose(bank[:, j, :], zp_cut[:, c : c + 1].to_broadcast([P, P]), identity[:])
            nc.scalar.copy(out=zp_table[:, a * BANK_SLOTS * P : (a + 1) * BANK_SLOTS * P], in_=bank[:].rearrange("p j n -> p (j n)"))
        zp_negated = keep.tile([P, S], F32, name="zp_negated")
        nc.scalar.activation(zp_negated[:], zp_table[:].indirect(offsets[:]), COPY, scale=-1.0)

        picked = keep.tile([P, S, PACK], BF16, name="picked", align_bytes=64)
        staged = keep.tile([P, 2, OWN], BF16, name="staged", align_bytes=64)
        own_end = OWN_FIRST + OWN
        own_runs = ((0, OWN - RUN), (OWN - RUN, OWN))

        def place(t, first, end):
            nc.scalar.activation(picked[:, first:end, t], planes[t][:].indirect(entries(first, end - first)), COPY)

        for t in range(2):
            nc.vector.tensor_copy(picked[:, :, t], planes[t][:].indirect(offsets[:]))
        place(2, 0, OWN_FIRST)
        place(2, own_end, S)
        nc.vector.tensor_copy(staged[:, 0, :], planes[2][:].indirect(entries(OWN_FIRST, OWN)))
        nc.vector.tensor_copy(out=picked[:, OWN_FIRST:own_end, 2], in_=staged[:, 0, :])
        for at, end in own_runs:
            nc.vector.tensor_copy(staged[:, 1, at:end], planes[3][:].indirect(entries(OWN_FIRST + at, end - at)))
        for first, end in ((0, OWN_FIRST), (own_end, 3 * STORE), (3 * STORE, S - RUN), (S - RUN, S)):
            place(3, first, end)
        for at, end in own_runs:
            nc.vector.tensor_copy(out=picked[:, OWN_FIRST + at : OWN_FIRST + end, 3], in_=staged[:, 1, at:end])

        def product(first, count, x_codes, x_scales):
            nc.vector.quantize_mx(
                out=x_codes.bitcast(FP8X4),
                scales=x_scales,
                in_=picked[:, first : first + count, :].rearrange("p c t -> p (c t)"),
            )
            y = ybanks.tile([P, count], F32, name=f"y{first}")
            nc.tensor.matmul_mx(
                out=y[:],
                lhsT=w_codes[:].bitcast(FP4X4),
                lhsT_scale=w_scales[:],
                rhs=x_codes.bitcast(FP8X4),
                rhs_scale=x_scales,
                start=True,
                stop=True,
            )
            return y

        results = [keep.tile([P, STORE], F32, name=f"result{j}", align_bytes=256) for j in range(S // STORE)]

        def correct(first, count, y):
            j, at = divmod(first, STORE)
            nc.vector.scalar_tensor_tensor(results[j][:, at : at + count], zp_negated[:, first : first + count], csum_col[:, 0:1], y[:], MULT, ADD)
            if at + count == STORE:
                nc.sync.dma_start(out=out[:, j * STORE : (j + 1) * STORE], in_=results[j][:])

        codes = [keep.tile([P, STORE], U32, name=f"codes{j}", align_bytes=64) for j in range(3)]
        scales = [keep.tile([P, STORE], U8, name=f"scales{j}", align_bytes=64) for j in range(3)]
        last_codes = keep.tile([P, RUN], U32, name="last_codes", align_bytes=64)
        last_scales = keep.tile([P, RUN], U8, name="last_scales", align_bytes=64)
        wide = [product(j * STORE, STORE, codes[j][:], scales[j][:]) for j in range(3)]
        narrow = [product(3 * STORE, RUN, last_codes[:], last_scales[:])]
        correct(0, STORE, wide[0])
        narrow.append(product(S - RUN, RUN, codes[0][:, :RUN], scales[0][:, :RUN]))
        for j in (1, 2):
            correct(j * STORE, STORE, wide[j])
        for j in range(2):
            correct(3 * STORE + j * RUN, RUN, narrow[j])
